import numpy as np, ml_dtypes
CORES = [66,74,82,90,194,202,210,218]
N = 8
BF = ml_dtypes.bfloat16
def gentries(a):
    return np.ascontiguousarray(a.reshape(8, 16, -1).transpose(0, 2, 1)).reshape(8, -1)
def gtable(e):
    e = np.asarray(e); return np.ascontiguousarray(e.reshape(8, -1, 16).transpose(0, 2, 1)).reshape(128, -1).astype(np.int32)
S, Q, T, CAP, RO = 1024, 4, 192, 96, 3
B = Q * S
def near(rng, c, a):
    return np.clip(np.take_along_axis(c, a[:, :, None, :], 3) + rng.integers(-40, 41, (N, 8, 16, T)), 0, 255)
def parts(rng):
    c = rng.integers(0, 256, (N, 8, 16, S)); g = rng.integers(-16, 16, (N, 8, 16, B))
    H = S >> 4; hub = np.argsort(rng.random((N, 8, S)), axis=2)[..., :H]
    i = np.minimum((H * rng.random((N, 8, 16 * S)) ** 2).astype(np.int64), H - 1)
    u = np.take_along_axis(hub, i, 2).reshape(N, 8, 16, S); u = np.where(rng.random(u.shape) < 0.5, u, rng.integers(0, S, u.shape))
    i = np.minimum((H * rng.random((N, 8, T)) ** 2).astype(np.int64), H - 1)
    a = np.take_along_axis(hub, i, 2); a = np.where(rng.random(a.shape) < 0.5, a, rng.integers(0, S, a.shape))
    h = rng.integers(0, Q, (N, 8, S)); e = rng.choice(np.array([0.1, 0.3, 0.6]), (N, 8, 1))
    f = np.where(rng.random((N, 8, S)) < e, 0, rng.integers(0, Q + 1, (N, 8, S)))
    return c, u, g, h, f, a, near(rng, c, a)
def pack(c, u, g, h, f, a, z):
    return {"xs": np.ascontiguousarray(c.reshape(N, 128, S)).astype(np.float32).astype(BF), "su": np.ascontiguousarray(u.reshape(N, 128, S)).astype(np.int32),
            "gs": np.ascontiguousarray(g.reshape(N, 128, B)).astype(np.float32).astype(BF), "hd0": h.astype(np.int32), "fl0": f.astype(np.int32),
            "a0": np.stack([gtable(v) for v in a]), "z0": np.ascontiguousarray(z.reshape(N, 128, T)).astype(np.float32).astype(BF)}
def setup_inputs(rng):
    return pack(*parts(rng))
def setup_inputs_room(rng):
    c, u, g, h, f, a, z = parts(rng); num = (CAP, CAP + 1, T, CAP - 1, 1, 0, CAP, CAP + 1)
    for r in range(N):
        for k in range(8):
            j = (r + k) % 8; o = rng.permutation(S)[:T]; a[r, k] = o
            full = rng.integers(1, Q + 1, T)
            if j in (3, 5, 6):
                full[:] = 1 if j == 5 else Q
                u[r, k] = np.arange(S)
            f[r, k, o] = np.where(rng.permutation(T) < num[j], 0, full)
    return pack(c, u, g, h, f, a, near(rng, c, a))
def setup_inputs_crowd(rng):
    c, u, g, h, f, a, z = parts(rng)
    for r in range(N):
        for k in range(8):
            j = (r + k) % 8
            if j == 7: continue
            o = np.concatenate([rng.permutation(np.array([0, S - 1])), 1 + rng.permutation(S - 2)])
            if j < 4:
                n = (1, 2, 5, 12)[j]; a[r, k] = o[rng.integers(0, n, T)]; u[r, k] = o[rng.integers(0, n, (16, S))]
            else:
                w = (Q, Q, Q + 1)[j - 4]; o = o[:(T + w - 1) // w]
                a[r, k] = rng.permutation(np.repeat(o, w)[:T]); f[r, k, o] = (Q, 0, 0)[j - 4]
    return pack(c, u, g, h, f, a, near(rng, c, a))
def setup_inputs_ties(rng):
    c, u, g, h, f, a, z = parts(rng); pro = rng.integers(2, 254, (8, 16, 3))
    for k in range(8):
        if k % 2 == 0:
            c[:, k] = pro[k][:, np.arange(S) % 3]; g[:, k] = 2 * rng.integers(0, 2, (N, 16, B)) - 1; f[:, k] = f[:, k] * (rng.random((N, S)) < 0.5)
            if k % 4 == 2:
                g[:, k] = g[:, k] * rng.integers(0, 2, (N, 1, B)); u[:, k, 0] = np.where(rng.random((N, S)) < 0.5, np.arange(S), u[:, k, 0])
        else:
            c[:, k] = c[:, k][..., np.arange(S) // 2 * 2]; g[:, k] = g[:, k][..., np.arange(B) & 31]
    z = near(rng, c, a); z[:, ::2] = np.take_along_axis(c[:, ::2], a[:, ::2, None, :], 3)
    return pack(c, u, g, h, f, a, z)
def setup_inputs_ends(rng):
    c, u, g, h, f, a, z = parts(rng)
    c = 255 * rng.integers(0, 2, c.shape); g = 31 * rng.integers(0, 2, g.shape) - 16; z = 255 * rng.integers(0, 2, z.shape)
    k = rng.integers(0, 3, (N, 8, 1, T)); z = np.where(k == 0, 0, np.where(k == 1, 255, z))
    p = rng.permutation(8)
    f[:, p[0]] = 0; f[:, p[1]] = Q; h[:, p[2]] = Q - 1; h[:, p[3]] = 0
    for j in (4, 5, 6):
        w = p[j]; cw = rng.integers(0, 2, (N, 16, S)); zw = 255 - rng.integers(0, 2, (N, 16, T)); f[:, w] = Q * rng.integers(0, 2, (N, S))
        if j < 6:
            two = np.argsort(rng.random((N, 16, B)), axis=1) < 2
            gw = np.where(two, -rng.integers(1, 9, (N, 16, B)), rng.integers(6, 16, (N, 16, B)))
            if j == 5: cw = 255 - cw; zw = 255 - zw; gw = -gw
            g[:, w] = gw
        c[:, w] = cw; z[:, w] = zw
    a[..., 0] = 0; a[..., 1] = S - 1; a[..., T - 2] = 0; a[..., T - 1] = S - 1
    u = np.where(rng.random(u.shape) < 0.3, (S - 1) * rng.integers(0, 2, u.shape), u)
    return pack(c, u, g, h, f, a, z)
def setup_inputs_spread(rng):
    c, u, g, h, f, a, z = parts(rng)
    c = np.minimum((256 * rng.random(c.shape) ** np.exp2(rng.uniform(-3, 3, (N, 8, 1, S)))).astype(np.int64), 255)
    z = np.minimum((256 * rng.random(z.shape) ** np.exp2(rng.uniform(-3, 3, (N, 8, 1, T)))).astype(np.int64), 255)
    g = np.clip(np.floor((rng.random(g.shape) * 2 - 1) * np.exp2(rng.uniform(-2, 4, (N, 8, 1, B)))).astype(np.int64), -16, 15)
    m = rng.permuted(np.tile(np.arange(S), (N, 8, 1)), axis=2)
    i = np.minimum((S * rng.random((N, 8, 16 * S)) ** rng.uniform(1, 5, (N, 8, 1))).astype(np.int64), S - 1); u = np.take_along_axis(m, i, 2).reshape(N, 8, 16, S)
    i = np.minimum((S * rng.random((N, 8, T)) ** rng.uniform(1, 5, (N, 8, 1))).astype(np.int64), S - 1); a = np.take_along_axis(m, i, 2)
    f = np.minimum(((Q + 1) * rng.random((N, 8, S)) ** np.exp2(rng.uniform(-2, 2, (N, 8, 1)))).astype(np.int64), Q)
    return pack(c, u, g, h, f, a, z)
def check_inputs(d):
    bad = []
    for k, lo, hi in (("xs", 0, 255), ("su", 0, S - 1), ("gs", -16, 15), ("hd0", 0, Q - 1), ("fl0", 0, Q), ("a0", 0, S - 1), ("z0", 0, 255)):
        v = np.asarray(d[k]).astype(np.float64)
        if not (np.all(v >= lo) and np.all(v <= hi) and np.all(v == np.floor(v))): bad.append("range of " + k)
    return bad
def reference(xs, su, gs, hd0, fl0, a0, z0):
    X = xs.astype(np.float32).astype(np.int64).reshape(N, 8, 16, S); U = su.astype(np.int64).reshape(N, 8, 16, S)
    G = gs.astype(np.float32).astype(np.int64).reshape(N, 8, 16, B); hd = hd0.astype(np.int64); fl = fl0.astype(np.int64)
    a = np.stack([gentries(v) for v in a0]).astype(np.int64); z = z0.astype(np.float32).astype(np.int64).reshape(N, 8, 16, T)
    low = np.tri(T, k=-1, dtype=bool); odd = 2 * np.arange(16)[:, None] + 1
    for t in range(RO):
        same = a[:, :, :, None] == a[:, :, None, :]
        place = np.sum(same & low, axis=3); count = np.sum(same, axis=3)
        ha = np.take_along_axis(hd, a, 2); fa = np.take_along_axis(fl, a, 2)
        pop = place < fa; slot = Q * a + ((ha + place) & (Q - 1))
        zn = np.clip(z + np.take_along_axis(G, slot[:, :, None, :], 3), 0, 255)
        s = np.take_along_axis(U, a[:, :, None, :], 3)
        c = np.take_along_axis(X, s.reshape(N, 8, 1, 16 * T), 3).reshape(N, 8, 16, 16, T)
        best = np.argmin(np.sum(np.abs(c - zn[:, :, :, None, :]), axis=2), axis=2)
        to = np.take_along_axis(s, best[:, :, None, :], 2)[:, :, 0]
        gone = np.minimum(count, fa)
        np.put_along_axis(hd, a, (ha + gone) & (Q - 1), 2); np.put_along_axis(fl, a, fa - gone, 2)
        ask = ~pop & (np.add.accumulate((~pop).astype(np.int64), axis=2) <= CAP)
        d = 1 + t % (N - 1); XR = np.roll(X, -d, axis=0); GR = np.roll(G, -d, axis=0)
        u = np.sum(odd * z, axis=2) & 4095
        ix = (((u * u) >> 5)[:, :, None, :] + odd * u[:, :, None, :]) & (B - 1)
        cand = np.take_along_axis(GR, ix.reshape(N, 8, 1, 16 * T), 3).reshape(N, 8, 16, 16, T)
        goal = np.take_along_axis(XR, a[:, :, None, :], 3)
        m = np.argmin(np.sum(np.abs(z[:, :, :, None, :] + cand - goal[:, :, :, None, :]), axis=2), axis=2)
        seg = np.take_along_axis(cand, m[:, :, None, None, :], 3)[:, :, :, 0]
        put = ask & (place - fa < Q)
        for r in range(N):
            for g in range(8):
                w = np.flatnonzero(put[r, g])
                G[r, g][:, slot[r, g, w]] = seg[r, g][:, w]
                np.add.at(fl[r, g], a[r, g, w], 1)
        a = np.where(pop, to, a); z = np.where(pop[:, :, None, :], zn, z)
    return {"yz": z.reshape(N, 128, T).astype(np.float32).astype(BF), "ya": a.astype(np.float32), "yh": hd.astype(np.float32), "yf": fl.astype(np.float32)}

@@ -1,0 +1,708 @@
+import numpy as np
+from concourse.bass import DstId, RemoteDMATransfer
+from concourse.mybir import dt, AluOpType, AxisListType, ActivationFunctionType
+
+A = AluOpType
+F = ActivationFunctionType
+
+SCRATCH = {}
+for _n, _c, _d in (
+    ("XS", 1024, "bfloat16"), ("SU", 1216, "int32"), ("BK", 4208, "bfloat16"), ("HFI", 1024, "int32"), ("HF", 1216, "bfloat16"),
+    ("MK", 9424, "bfloat16"), ("A0", 12, "int32"), ("aF", 12, "float32"), ("Z0", 192, "bfloat16"), ("Z1", 192, "bfloat16"),
+    ("Z2", 192, "bfloat16"), ("Z3", 192, "bfloat16"), ("ZQ0", 576, "int32"), ("ZQ1", 576, "int32"),
+    ("QL0", 96, "int32"), ("QL1", 96, "int32"), ("AL0", 96, "bfloat16"), ("AL1", 96, "bfloat16"),
+    ("ONE", 1536, "bfloat16"), ("A16", 192, "bfloat16"), ("A16F", 128, "float32"), ("BOT", 128, "bfloat16"),
+    ("BO", 128, "bfloat16"), ("BOH", 128, "float16"), ("BOHK", 128, "float16"),
+    ("B16", 128, "bfloat16"), ("BM16", 128, "bfloat16"), ("BN", 128, "bfloat16"), ("B64K", 128, "bfloat16"),
+    ("ID", 128, "bfloat16"), ("IDN", 128, "bfloat16"), ("IDH", 128, "float16"), ("IDHN", 128, "float16"), ("IDF", 128, "float32"),
+    ("KLH", 12, "float16"), ("L0", 128, "bfloat16"), ("L16", 128, "bfloat16"), ("U0", 128, "bfloat16"), ("U16", 128, "bfloat16"),
+    ("TRI0", 128, "bfloat16"), ("TRI", 128, "bfloat16"), ("ZER", 1178, "bfloat16"), ("SELJ", 2048, "bfloat16"),
+    ("DC", 6, "float32"), ("MASK", 192, "float32"), ("MSK16", 192, "float32"), ("RSTB", 256, "bfloat16"),
+    ("RST", 256, "float32"), ("RBIG", 256, "float32"), ("IC", 256, "bfloat16"), ("SEL", 1536, "bfloat16"), ("IOT", 32, "int32"),
+    ("RI", 16, "uint16"), ("R15", 16, "uint16"), ("CST", 20, "float32"), ("CSR", 20, "float32"), ("DMK", 12, "float32"),
+    ("K1K", 12, "float32"), ("MCOL", 1, "float32"), ("WU", 128, "float16"), ("WU2", 128, "float16"), ("OROW", 128, "float32"),
+    ("ON12", 12, "float32"), ("ST1", 192, "bfloat16"), ("ST2", 192, "bfloat16"), ("ST3", 192, "bfloat16"),
+    ("G0", 192, "float16"), ("ARH", 192, "float16"), ("W", 192, "float32"), ("AS", 192, "float32"), ("AO", 12, "uint16"),
+    ("HFG", 192, "bfloat16"), ("EQ", 1248, "bfloat16"), ("WV", 192, "float32"),
+    ("SV", 192, "int32"), ("T1", 192, "bfloat16"), ("PKS", 192, "float32"), ("OFQ", 12, "uint16"),
+    ("ZS", 192, "float16"), ("SGM", 192, "float16"), ("SGU", 192, "uint16"), ("ZT", 256, "bfloat16"),
+    ("CG", 3072, "bfloat16"), ("AD", 3072, "bfloat16"), ("SK", 256, "float32"), ("KE", 256, "float32"), ("H", 256, "bfloat16"),
+    ("P", 192, "float16"), ("AFIN", 192, "float32"), ("NW", 192, "float32"), ("NS", 192, "float32"), ("GV", 192, "bfloat16"),
+    ("LF", 320, "float32"), ("LI", 160, "int32"), ("LU", 96, "uint16"), ("BLK", 12, "bfloat16"), ("SC", 12, "bfloat16"), ("PK12", 12, "float16"),
+    ("ZI", 96, "int32"), ("ZH", 96, "float16"), ("QW", 96, "float32"), ("QS", 96, "int32"), ("WQ", 96, "bfloat16"), ("WC", 96, "bfloat16"),
+    ("WT", 128, "bfloat16"), ("U5", 576, "int32"), ("COU", 96, "uint16"), ("COF", 96, "float32"), ("CA", 1536, "bfloat16"),
+    ("AA", 1536, "bfloat16"), ("KQ", 128, "int32"), ("K8", 8, "int32"),
+    ("LT", 128, "float32"), ("ANS0", 96, "bfloat16"), ("ANS1", 96, "bfloat16"), ("RW", 96, "float32"), ("RS", 96, "int32"),
+    ("OF", 128, "float32"), ("OI", 256, "int32"),
+):
+    SCRATCH[_n] = ("sbuf", [128, _c], _d)
+for _k in range(8):
+    SCRATCH["b%d" % _k] = ("psum", [128, 512], "float32")
+
+LOADS = ["a0", "z0", "fl", "hd", "su", "gs", "xs", "zero", "yz", "ya", "yh", "yf"]
+SEMAPHORES = ["cv", "ct", "ca", "cg"] + ["d_" + n for n in LOADS] + ["q0", "q1", "an0", "an1", "sent"]
+
+SCH = ((2, 3, 4, 5), (2, 3, 4, 5), (3, 4, 5))
+ANS_S = (1, 2)
+ANS_ORDER = (0, 2, 1)
+
+CYC, GATHER, SCATTER, PE_US, DMA_US, WAKE_US, TOL_US = 0.00104, 1.56, 3.8, 0.00072, 2.5, 0.07, 0.04
+WAYS = ((1.0, 1.0, 1.0, 4.0), (1.25, 1.2, 1.0, 3.0), (0.9, 0.9, 1.2, 5.5))
+TRIES, MOVES, SEED = 300, 7000, 0
+BYTES = {"float32": 4, "int32": 4, "bfloat16": 2, "float16": 2, "uint16": 2}
+SETTLED = {}
+
+
+def settle(ops):
+    if "order" in SETTLED:
+        return SETTLED["order"]
+    n = len(ops)
+    last, pred = {}, [{} for _ in range(n)]
+    for i, (q, fn, rr, ww, sem, tot, us, lat) in enumerate(ops):
+        for w, regs in ((False, rr), (True, ww)):
+            for nm, lo, hi in regs:
+                ps = SCRATCH.get(nm, ("dram",))[0] == "psum"
+                for (l2, h2, w2, j) in last.get(nm, ()):
+                    over = h2 > lo and hi > l2
+                    if j != i and (ps or ((w or w2) and over)):
+                        waits = ops[j][0] != q or sem or ops[j][4] or (w2 and not w and over)
+                        pred[i][j] = max(pred[i].get(j, 0.0), WAKE_US if waits else 0.0)
+        for w, regs in ((False, rr), (True, ww)):
+            for nm, lo, hi in regs:
+                last.setdefault(nm, []).append((lo, hi, w, i))
+    pred = [sorted(p.items()) for p in pred]
+    succ = [[] for _ in range(n)]
+    for i in range(n):
+        for j, wk in pred[i]:
+            succ[j].append((i, wk))
+    cost = []
+    for fv, fa, ft, fl in WAYS:
+        f = {"v": fv, "a": fa, "t": ft}
+        cost.append([(o[6] * f.get(o[0], 1.0), fl if o[5] < 0 else o[7]) for o in ops])
+    base = [0.0] * n
+    for i in range(n - 1, -1, -1):
+        base[i] = cost[0][i][0] + max([0.0] + [cost[0][i][1] + wk + base[k] for k, wk in succ[i]])
+
+    def listed(prio):
+        left, at = [len(p) for p in pred], [0.0] * n
+        free = {q: 0.0 for q in "vtagsr"}
+        ready = {q: set() for q in "vtagsr"}
+        for i in range(n):
+            if left[i] == 0:
+                ready[ops[i][0]].add(i)
+        order = []
+        while len(order) < n:
+            bq, bs = None, 1e9
+            for q, r in ready.items():
+                if r:
+                    s = max(free[q], min(at[i] for i in r))
+                    if s < bs:
+                        bq, bs = q, s
+            i = max((k for k in ready[bq] if at[k] <= bs + TOL_US), key=lambda k: (prio[k], -k))
+            ready[bq].remove(i)
+            order.append(i)
+            us, lat = cost[0][i]
+            free[bq] = end = max(free[bq], at[i]) + us
+            end += lat
+            for k, wk in succ[i]:
+                if end + wk > at[k]:
+                    at[k] = end + wk
+                left[k] -= 1
+                if left[k] == 0:
+                    ready[ops[k][0]].add(k)
+        return order
+
+    def ends(order):
+        tot = 0.0
+        for cs in cost:
+            done, free = [0.0] * n, {q: 0.0 for q in "vtagsr"}
+            for i in order:
+                us, lat = cs[i]
+                s = free[ops[i][0]]
+                for j, wk in pred[i]:
+                    if done[j] + wk > s:
+                        s = done[j] + wk
+                free[ops[i][0]] = s + us
+                done[i] = s + us + lat
+            tot += max(done)
+        return tot / len(cost)
+
+    rng = np.random.default_rng(SEED)
+    prio = list(base)
+    best = listed(base)
+    end = ends(best)
+    for _ in range(TRIES):
+        p = list(prio)
+        for k in rng.integers(0, n, int(rng.integers(1, 25))):
+            p[int(k)] += float(rng.normal() * 3.0)
+        o = listed(p)
+        e = ends(o)
+        if e <= end:
+            best, prio, end = o, p, e
+    pos = [0] * n
+    for x, i in enumerate(best):
+        pos[i] = x
+    cur, cend = list(best), end
+    for step in range(MOVES):
+        i = int(rng.integers(n))
+        if ops[i][0] == "r":
+            continue
+        lo = max([pos[j] for j, wk in pred[i]], default=-1) + 1
+        hi = min([pos[k] for k, wk in succ[i]], default=n) - 1
+        lo, hi = max(lo, pos[i] - 150), min(hi, pos[i] + 150)
+        if hi <= lo:
+            continue
+        x = int(rng.integers(lo, hi + 1))
+        if x == pos[i]:
+            continue
+        o = list(cur)
+        o.pop(pos[i])
+        o.insert(x, i)
+        e = ends(o)
+        if e <= cend + 0.05 * (1.0 - step / MOVES) * float(rng.random()) ** 3:
+            for y in range(min(x, pos[i]), max(x, pos[i]) + 1):
+                pos[o[y]] = y
+            cur, cend = o, e
+            if e < end:
+                best, end = o, e
+    SETTLED["order"], SETTLED["end"] = best, end
+    return best
+
+
+def rank_program(g, core, T, topo):
+    rank = T.rank_of(core)
+    if rank is None:
+        return
+    eng = {"v": g.vector, "t": g.tensor, "a": g.scalar, "g": g, "s": g.sync}
+    csem = {"v": "cv", "t": "ct", "a": "ca", "g": "cg"}
+    count = {"v": 0, "t": 0, "a": 0, "g": 0}
+    known = {q: {} for q in ("v", "t", "a", "g", "s", "r")}
+    hist = {}
+
+    def need(q, reads, writes, away):
+        toks = []
+        for w, regs in ((False, reads), (True, writes)):
+            for nm, lo, hi in regs:
+                ps = SCRATCH.get(nm, ("dram",))[0] == "psum"
+                for (l2, h2, w2, q2, sem, val, clk, away2) in hist.get(nm, ()):
+                    over = h2 > lo and hi > l2
+                    if q2 == q and not away and not away2:
+                        if w2 and not w and over:
+                            toks.append((sem, val, clk))
+                    elif ps or (over and (w or w2)):
+                        toks.append((sem, val, clk))
+        k = known[q]
+        toks.sort(key=lambda t: -t[1])
+        for sem, val, clk in toks:
+            if k.get(sem, 0) >= val:
+                continue
+            eng[q].wait_ge(T.sem[sem], val)
+            for s, v in clk.items():
+                if k.get(s, 0) < v:
+                    k[s] = v
+
+    def note(q, reads, writes, sem, val, away):
+        clk = dict(known[q])
+        clk[sem] = max(clk.get(sem, 0), val)
+        for nm, lo, hi in writes:
+            old = hist.get(nm, [])
+            hist[nm] = [e for e in old if not (lo <= e[0] and e[1] <= hi)] + [(lo, hi, True, q, sem, val, clk, away)]
+        for nm, lo, hi in reads:
+            old = hist.setdefault(nm, [])
+            hist[nm] = [e for e in old if not (not e[2] and e[3] == q and lo <= e[0] and e[1] <= hi and not e[7])] \
+                + [(lo, hi, False, q, sem, val, clk, away)]
+
+    def flat(xs):
+        out = []
+        for x in xs:
+            out += x[1] if isinstance(x[1], list) else [x[1]]
+        return out
+
+    ops = []
+
+    def run(q, fn, reads, writes, us):
+        ops.append((q, fn, flat(reads), flat(writes), None, 0, us, 0.0))
+
+    def dma(q, name, out, in_, total=16):
+        rr = [in_[1]] if in_[1] else []
+        ww = [out[1]] if out[1] else []
+        ops.append((q, lambda: eng[q].dma_start(out[0], in_[0]), rr, ww, "d_" + name, total, 0.06, DMA_US))
+
+    def c(name, lo=0, hi=None, step=1, p0=0, p1=128, ps=1):
+        hi = SCRATCH[name][1][1] if hi is None else hi
+        t = T[name]
+        if step == 1:
+            ap = t[p0:p1, lo:hi] if ps == 1 else t[p0:p1:ps, lo:hi]
+        else:
+            ap = t[p0:p1, lo:hi:step]
+        return (ap, (name, lo, hi), len(range(lo, hi, step)), BYTES[SCRATCH[name][2]], SCRATCH[name][0])
+
+    def ind(win, off):
+        return (win[0].indirect(off[0]), [win[1], off[1]], 16 * off[2], 4, "list")
+
+    def ext(ap):
+        return (ap, None)
+
+    def val(x):
+        return x[0] if isinstance(x, tuple) else x
+
+    def cyc(out, ins, per):
+        n = max(x[2] for x in ins)
+        if out[4] == "list":
+            return 0.05 + n * SCATTER * CYC
+        if any(x[4] == "list" for x in ins):
+            return 0.05 + n * GATHER * CYC
+        return max(64, n * per) * CYC
+
+    def half(*xs):
+        return 0.5 if all(x[3] == 2 for x in xs) else 1.0
+
+    def copy(out, in_):
+        if out[4] == "list":
+            rd, wr = [in_, (0, out[1][1])], [(0, out[1][0])]
+        else:
+            rd, wr = [in_], [out]
+        run("v", lambda: g.vector.tensor_copy(out[0], in_[0]), rd, wr, cyc(out, [in_], half(out, in_)))
+
+    def tt(out, a, b, op):
+        run("v", lambda: g.vector.tensor_tensor(out[0], a[0], b[0], op), [a, b], [out],
+            cyc(out, [a, b], 1.0 if "psum" in (a[4], b[4]) else 2.0))
+
+    def ts(out, a, s1, op0, s2=None, op1=None):
+        rd = [a] + [x for x in (s1, s2) if isinstance(x, tuple)]
+        us = cyc(out, [a], half(out, a))
+        if op1 is None:
+            run("v", lambda: g.vector.tensor_scalar(out[0], a[0], val(s1), None, op0), rd, [out], us)
+        else:
+            run("v", lambda: g.vector.tensor_scalar(out[0], a[0], val(s1), val(s2), op0, op1), rd, [out], us)
+
+    def scan(out, d0, d1, init, o0, o1):
+        run("v", lambda: g.vector.tensor_tensor_scan(out[0], d0[0], d1[0], init, o0, o1), [d0, d1], [out], cyc(out, [d1], 1.0))
+
+    def fill(x, v):
+        run("v", lambda: g.vector.memset(x[0], v), [], [x], cyc(x, [x], half(x)))
+
+    def mm(out, lhsT, rhs, start, stop):
+        us = PE_US * max(64, rhs[2]) * (4 if rhs[3] == 4 else 1)
+        run("t", lambda: g.tensor.matmul(out[0], lhsT[0], rhs[0], start, stop), [lhsT, rhs], [out], us)
+
+    def act(out, in_, func, bias=0.0, scale=1.0):
+        run("a", lambda: g.scalar.activation(out[0], in_[0], func, bias=bias, scale=scale), [in_], [out], cyc(out, [in_], 1.0))
+
+    def iota(out, pattern, base, cm):
+        us = 0.13 + 2 * out[2] * CYC
+        if SCRATCH[out[1][0]][2] == "int32":
+            run("g", lambda: g.iota(out[0], pattern, base, cm), [], [out], us)
+        else:
+            run("g", lambda: g.iota(out[0], pattern, base, cm, allow_small_or_imprecise_dtypes=True), [], [out], us)
+
+    def asel(out, in_, pattern, cmp, fillv, base, cm):
+        run("g", lambda: g.affine_select(out[0], in_[0], pattern, cmp, fillv, base, cm), [in_], [out], 0.17 + 2 * out[2] * CYC)
+
+    dma("s", "a0", c("A0"), ext(T.a0[:]))
+    dma("a", "z0", c("Z0"), ext(T.z0[:]))
+    fill(c("ONE", 0, 256), 1.0)
+    run("v", lambda: g.vector.memset(T.HFI[:], 0), [], [c("HFI"), (0, ("HFI1", 0, 1024))], 1024 * CYC)
+    dma("s", "fl", c("HFI", p0=0, ps=16), ext(T.fl0[:]))
+    ops.append(("s", lambda: g.sync.dma_start(T.HFI[1:128:16, :], T.hd0[:]), [], [("HFI1", 0, 1024)], "d_hd", 16, 0.06, DMA_US))
+    dma("s", "su", c("SU", 0, 1024), ext(T.su[:]))
+    dma("a", "gs", c("BK", 0, 4096), ext(T.gs[:]))
+    dma("s", "xs", c("XS"), ext(T.xs[:]))
+
+    asel(c("A16", p1=16), c("ONE", 0, 192, p1=16), [[0, 12], [-1, 16]], A.is_equal, 0.0, 0, 1)
+    asel(c("BOT"), c("ONE", 0, 128), [[-16, 8], [0, 16]], A.is_ge, 0.0, 0, 1)
+    asel(c("BO"), c("BOT"), [[16, 8], [0, 16]], A.is_ge, 0.0, 15, -1)
+    iota(c("IOT", 0, 16), [[1, 16]], 0, 0)
+    iota(c("IOT", 16, 32), [[16, 16]], 15, 0)
+    asel(c("L0"), c("BO"), [[1, 128]], A.is_gt, 0.0, 0, -1)
+    asel(c("U0"), c("BO"), [[-1, 128]], A.is_ge, 0.0, 0, 1)
+    iota(c("CST", 0, 1, p1=16), [[0, 1]], 1, 2)
+    iota(c("CST", 1, 13, p1=16), [[16, 12]], 193, 1)
+    iota(c("CST", 13, 19, p1=16), [[16, 6]], 4112, 1)
+    fill(c("LF", 312, 313), 0.0)
+    asel(c("LF", 313, 314), c("LF", 312, 313), [[0, 1]], A.not_equal, 240.0, 0, 1)
+    asel(c("CST", 19, 20), c("LF", 313, 314), [[0, 1]], A.not_equal, -16.0, -1, 1)
+    asel(c("RSTB"), c("ONE", 0, 256), [[0, 16], [1, 16]], A.not_equal, 0.0, 0, 0)
+    asel(c("TRI0"), c("BO"), [[-1, 128]], A.is_gt, 0.0, 0, 1)
+    asel(c("ID"), c("ONE", 0, 128), [[-1, 128]], A.is_equal, 0.0, 0, 1)
+    fill(c("ZER"), 0.0)
+    mm(c("b0", 0, 192), c("A16", 0, 128, p1=16), c("A16", p1=16), True, True)
+    copy(c("RI"), c("IOT", 0, 16))
+    copy(c("MASK"), c("b0", 0, 192))
+    copy(c("aF"), c("A0"))
+    copy(c("AO"), c("A0"))
+    tt(c("G0"), ind(c("aF"), c("RI", 0, 12)), c("MASK"), A.mult)
+    copy(c("BOH"), c("BO"))
+    copy(c("R15"), c("IOT", 16, 32))
+    mm(c("b5", 0, 192), c("BOH"), c("G0"), True, True)
+    act(c("L16"), c("L0"), F.Copy, scale=16.0)
+    act(c("U16"), c("U0"), F.Copy, scale=16.0)
+    act(c("B16"), c("BO"), F.Copy, scale=16.0)
+    act(c("BM16"), c("BO"), F.Copy, scale=-1.0 / 16)
+    act(c("A16F", p1=16), c("A16", 0, 128, p1=16), F.Copy)
+    mm(c("b2", 0, 20), c("A16F", p1=16), c("CST", p1=16), True, True)
+    act(c("CSR"), c("b2", 0, 20), F.Copy)
+    act(c("RST"), c("RSTB"), F.Copy)
+    act(c("TRI"), c("TRI0"), F.Copy, scale=-1.0)
+    act(c("BN"), c("BO"), F.Copy, scale=-256.0)
+    for k in range(8):
+        dma("s", "zero", c("MK", 1178 * k, 1178 * k + 1178), c("ZER"), 160)
+    for k in range(2):
+        dma("s", "zero", c("SELJ", 1024 * k, 1024 * k + 1024), c("ZER", 0, 1024), 160)
+
+    KL = c("CSR", 1, 13)
+
+    def consts_mid():
+        run("v", lambda: g.vector.tensor_scalar(T.HF[:, 0:1024], T.HFI[:], T.CSR[:, 19:20], None, A.mult),
+            [c("HFI"), c("CSR", 19, 20), (0, ("HFI1", 0, 1024))], [c("HF", 0, 1024)], 1024 * CYC)
+        fill(c("ON12"), 1.0)
+        copy(c("IDH"), c("ID"))
+        ts(c("IDHN"), c("ID"), -1.0, A.mult)
+        copy(c("KLH"), KL)
+        ts(c("BOHK"), c("BO"), 1024.0, A.mult)
+        for n in ("ZQ0", "ZQ1"):
+            fill(c(n, 0, 96), 16128)
+        fill(c("BK", 4096, 4208), 0.0)
+        ts(c("K1K"), KL, 831.0, A.add)
+        fill(c("ONE", 256, 1536), 1.0)
+        iota(c("OROW"), [[0, 8], [2, 16]], 1, 0)
+        iota(c("IC", p1=1), [[0, 16], [1, 16]], 0, 0)
+        asel(c("SEL"), c("ONE"), [[-1, 96], [0, 16]], A.is_equal, 0.0, 0, 1)
+        act(c("IDN"), c("ID"), F.Copy, scale=-1.0)
+
+    def consts_last():
+        act(c("RBIG"), c("RST"), F.Copy, scale=-2e9, bias=1e9)
+        act(c("SK"), c("RST"), F.Copy)
+        act(c("KE"), c("RST"), F.Copy)
+        act(c("B64K"), c("BO"), F.Copy, scale=65536.0)
+        act(c("IDF"), c("ID"), F.Copy)
+        act(c("DC"), c("BO", 0, 96, 16), F.Copy)
+        act(c("MCOL"), c("CSR", 0, 1), F.Copy, scale=2048.0, bias=-2048.0 - 248.0 * 65536.0)
+        act(c("DMK"), KL, F.Copy, bias=9023.0)
+        ts(c("WU"), c("BO"), c("CSR", 0, 1), A.mult)
+        fill(c("K8"), 0)
+        fill(c("HF", 1024, 1216), 0.0)
+        tt(c("WU2"), c("WU"), c("OROW"), A.mult)
+
+    def consts_tail():
+        act(c("MSK16"), c("MASK"), F.Copy, scale=16.0)
+        for k in range(3):
+            act(c("ST%d" % (k + 1)), c("ONE", 0, 192), F.Copy, scale=float(k + 1))
+
+    def consts_out():
+        for j in range(16):
+            act(c("SELJ", 128 * j + j, 128 * j + 128, 16), c("BO", 0, 128, 16), F.Copy, scale=1.0 / 16)
+
+    def lf(k, n=12):
+        return c("LF", 12 * k, 12 * k + n)
+
+    def li(k, n=12):
+        return c("LI", 12 * k, 12 * k + n)
+
+    def lu(k, n=12):
+        return c("LU", 12 * k, 12 * k + n)
+
+    VL = c("SV", 15, 192, 16)
+
+    def aL(t):
+        return c("aF") if t == 0 else c("AS", 15, 192, 16)
+
+    nsent = [0]
+
+    def send(dst, out, in_, sem):
+        rid, pid = topo.addr(T.cores[dst], core)
+        nsent[0] += len(topo.engines(core, T.cores[dst]))
+        ops.append(("g", lambda: g.remote_dma(out, in_[0], T.sem[sem], T.sem.sent, pid, rid, topo.mask(core, T.cores[dst])),
+                    [in_[1]], [("sent " + sem, 0, 1)], None, -1, 0.3, 0.0))
+
+    def landed(buf, sem, src):
+        n = len(topo.engines(T.cores[src], core))
+        ops.append(("r", None, [("sent " + sem, 0, 1)], [(buf, 0, SCRATCH[buf][1][1])], sem, n, 0.0, 0.0))
+
+    def places(t):
+        ask = t < 2
+        A5 = c("b5", 0, 192)
+        copy(c("ARH"), A5)
+        if t > 0:
+            tt(c("W"), A5, c("MASK"), A.mult)
+            scan(c("AS"), c("RST", 0, 192), c("W"), 0.0, A.mult, A.add)
+            copy(c("AO"), aL(t))
+        else:
+            consts_mid()
+        act(c("HFG"), ind(c("HF", 0, 1024), c("AO")), F.Copy)
+        V = c("b3", 0, 192)
+        o = 0
+        for k in range(12):
+            n = 192 - 16 * k
+            col = c("aF", k, k + 1) if t == 0 else c("AS", 16 * k + 15, 16 * k + 16)
+            ts(c("EQ", o, o + n), c("ARH", 16 * k, 192), col, A.is_equal)
+            if k == 0:
+                mm(V, c("L16"), c("EQ", 0, 192), True, False)
+                mm(c("b3", 16, 192), c("U16"), c("EQ", 16, 192), False, False)
+            else:
+                mm(c("b3", 16 * k, 16 * k + 16), c("L16"), c("EQ", o, o + 16), False, False)
+                if k < 11:
+                    mm(c("b3", 16 * k + 16, 192), c("B16"), c("EQ", o + 16, o + n), False, False)
+            o += n
+        mm(V, c("BM16"), c("HFG"), False, True)
+        copy(c("SU", 1024, 1216), A5)
+        act(lf(1), aL(t), F.Copy, scale=4.0)
+        act(lf(8), aL(t), F.Copy, scale=9.0, bias=4.0)
+        tt(lf(19), aL(t), c("K1K"), A.subtract)
+        tt(c("WV"), V, c("MASK"), A.mult)
+        if ask:
+            act(c("T1"), c("WV"), F.Relu, bias=63.0, scale=-1.0)
+            PK = c("b4", 0, 192)
+            mm(PK, c("ID"), c("Z%d" % t), True, False)
+            mm(PK, c("BOHK"), c("ARH"), False, False)
+            mm(PK, c("BN"), c("T1"), False, True)
+            act(c("PKS"), PK, F.Copy, bias=256.0 * 1008.0)
+        scan(c("SV"), c("RST", 0, 192), c("WV"), 0.0, A.mult, A.add)
+        ts(c("BLK"), VL, 0.0, A.is_ge)
+        scan(c("SC"), c("ON12"), c("BLK"), 0.0, A.mult, A.add)
+        tt(c("PK12"), c("BLK"), KL, A.mult)
+        CUM = c("b6", 0, 12)
+        mm(CUM, c("TRI"), c("BLK"), True, False)
+        mm(CUM, c("BO"), c("SC"), False, False)
+        mm(CUM, c("IDH"), c("KLH"), False, False)
+        mm(CUM, c("IDHN"), c("PK12"), False, True)
+        ts(li(0), VL, 4, A.arith_shift_right)
+        tt(lf(21), c("BLK"), c("K1K"), A.mult)
+        act(lf(2), c("BLK"), F.Copy, scale=4096.0)
+        tt(li(1), li(0), VL, A.add)
+        tt(lf(21), lf(21), aL(t), A.max)
+        if ask:
+            ts(c("OFQ"), CUM, -1.0, A.add)
+            copy(ind(c("ZQ%d" % t), c("OFQ")), c("PKS"))
+        act(lf(3), CUM, F.Abs, bias=-144.5)
+        if ask:
+            send((rank + 1 + t) % 8, T["QL%d" % t][:], c("ZQ%d" % t, 0, 96), "q%d" % t)
+        ts(li(2), li(1), 3, A.bitwise_and)
+        copy(lu(7), lf(21))
+        tt(lf(4), lf(1), li(2), A.add)
+        tt(lf(5), lf(4), lf(2), A.max)
+        copy(lu(0), lf(5))
+
+    def pop_front(t):
+        Z, Z1 = c("Z%d" % t), c("Z%d" % (t + 1))
+        tt(c("ZS"), ind(c("BK", 0, 4112), lu(0)), Z, A.add)
+        copy(c("SGU"), ind(c("SU"), lu(7)))
+        ts(Z1, c("ZS"), 0.0, A.max, 255.0, A.min)
+        for h in range(2):
+            mm(c("b4", 128 * h, 128 * h + 128, p1=96), c("Z%d" % (t + 1), 96 * h, 96 * h + 96), c("IDN"), True, True)
+        act(c("ZT", p1=96), c("b4", 0, 256, p1=96), F.Copy)
+
+    def pop_gathers(t):
+        for k in range(6):
+            o, i = c("CG", 512 * k, 512 * k + 512), ind(c("XS"), c("SGU", 32 * k, 32 * k + 32))
+            if k in SCH[t]:
+                act(o, i, F.Copy)
+            else:
+                copy(o, i)
+        for k in range(6):
+            D = c("b%d" % (k % 3))
+            mm(D, c("ZT", 128 * (k // 3), 128 * (k // 3) + 128, p1=96), c("SEL", 512 * (k % 3), 512 * (k % 3) + 512, p1=96), True, False)
+            mm(D, c("ID"), c("CG", 512 * k, 512 * k + 512), False, True)
+            act(c("AD", 512 * k, 512 * k + 512), D, F.Abs)
+        copy(c("SGM"), c("SGU"))
+
+    def pop_dist(t):
+        for h in range(2):
+            b = ("b3", "b4")[h]
+            mm(c(b, 0, 128, p1=96), c("ONE", 0, 96, p1=1), c("IC", 0, 128, p1=1), True, False)
+            for i in range(16):
+                mm(c(b, i, 128, 16, p1=96), c("AD", 1536 * h + i, 1536 * h + 1536, 16), c("B16", 0, 128, 16), False, i == 15)
+
+    def pop_min(t):
+        for h in range(2):
+            b = ("b3", "b4")[h]
+            act(c("KE", 128 * h, 128 * h + 128, p1=96), c(b, 0, 128, p1=96), F.Copy)
+            scan(c("SK", 128 * h, 128 * h + 128, p1=96), c("RBIG", 0, 128, p1=96), c(b, 0, 128, p1=96), 1e9, A.max, A.min)
+
+    def pop_hot(t):
+        tt(c("H"), ind(c("SK"), c("R15")), c("KE"), A.is_equal)
+        for h in range(2):
+            mm(c("b7", 96 * h, 96 * h + 96), c("H", 128 * h, 128 * h + 128, p1=96), c("ID", 0, 96, p1=96), True, True)
+
+    def pop_move(t):
+        tt(c("P"), c("b7", 0, 192), c("SGM"), A.mult)
+        mm(c("b5", 0, 192), c("BOH"), c("P"), True, True)
+
+    def answer_front(t):
+        QL = "QL%d" % t
+        landed(QL, "q%d" % t, (rank - 1 - t) % 8)
+        u = lambda k: c("U5", 96 * k, 96 * k + 96)
+        ts(c("ZI"), c(QL), 255, A.bitwise_and)
+        copy(c("ZH"), c("ZI"))
+        tt(c("QW"), c(QL), c("MASK", 0, 96), A.mult)
+        scan(c("QS"), c("RST", 0, 96), c("QW"), 0.0, A.mult, A.add)
+        mm(c("b7", 0, 96), c("WU"), c("ZH"), True, True)
+        mm(c("b7", 96, 192), c("WU2"), c("ZH"), True, True)
+        ts(li(3, 6), c("QS", 15, 96, 16), 14, A.arith_shift_right)
+        copy(lu(1, 6), li(3, 6))
+        tt(c("WQ"), ind(c("XS"), lu(1, 6)), c("ZI"), A.subtract)
+        copy(u(0), c("b7", 0, 96))
+        ts(c("WC"), c("WQ"), -16.0, A.max, 15.0, A.min)
+        ts(u(1), u(0), 4095, A.bitwise_and)
+        mm(c("b6", 128, 256, p1=96), c("WC"), c("IDN"), True, True)
+        act(c("WT", p1=96), c("b6", 128, 256, p1=96), F.Copy)
+        tt(u(2), u(1), u(1), A.mult)
+        ts(u(3), u(2), 5, A.arith_shift_right)
+        tt(u(4), c("b7", 96, 192), u(3), A.add)
+        ts(u(5), u(4), 4095, A.bitwise_and)
+        copy(c("COU"), u(5))
+
+    def answer_gathers(t):
+        for k in range(3):
+            o, i = c("CA", 512 * k, 512 * k + 512), ind(c("BK", 0, 4096), c("COU", 32 * k, 32 * k + 32))
+            if k in ANS_S:
+                act(o, i, F.Copy)
+            else:
+                copy(o, i)
+        ts(c("COF"), c("U5", 480, 576), c("MCOL"), A.add)
+        for k in ANS_ORDER:
+            D = c("b%d" % k)
+            mm(D, c("WT", p1=96), c("SEL", 512 * k, 512 * k + 512, p1=96), True, False)
+            mm(D, c("ID"), c("CA", 512 * k, 512 * k + 512), False, True)
+            act(c("AA", 512 * k, 512 * k + 512), D, F.Abs)
+
+    def answer_dist(t):
+        mm(c("b6", 0, 128, p1=96), c("COF"), c("IDF"), True, False)
+        for m in range(16):
+            mm(c("b6", m, 128, 16, p1=96), c("AA", m, 1536, 16), c("B64K", 0, 128, 16), False, m == 15)
+
+    def answer_list(t):
+        scan(c("KQ", p1=96), c("RBIG", 0, 128, p1=96), c("b6", 0, 128, p1=96), 1e9, A.max, A.min)
+        ts(c("K8", p1=96), c("KQ", 15, 128, 16, p1=96), 4095, A.bitwise_and)
+        tt(c("LT"), ind(c("K8"), c("RI", 0, 8)), c("MASK", 0, 128), A.mult)
+        mm(c("b6", 256, 262), c("LT", p1=96), c("DC", p1=96), True, True)
+
+    def answer_send(t):
+        copy(lu(2, 6), c("b6", 256, 262))
+        ANS = c("ANS%d" % t)
+        copy(ANS, ind(c("BK", 0, 4096), lu(2, 6)))
+        send((rank - 1 - t) % 8, T["AL%d" % t][:], ANS, "an%d" % t)
+
+    def refill_list(t):
+        u6 = lambda k: c("LI", 48 + 6 * k, 54 + 6 * k)
+        tt(c("RW"), c("ZQ%d" % t, 0, 96), c("MASK", 0, 96), A.mult)
+        scan(c("RS"), c("RST", 0, 96), c("RW"), 0.0, A.mult, A.add)
+        PL = c("RS", 15, 96, 16)
+        ts(u6(0), PL, 8, A.arith_shift_right, 63, A.bitwise_and)
+        ts(u6(1), PL, 14, A.arith_shift_right)
+        ts(u6(2), u6(0), 4, A.arith_shift_right)
+        ts(lf(12, 6), u6(0), 62.0, A.is_ge)
+        tt(u6(3), u6(0), u6(2), A.add)
+        ts(lf(13, 6), u6(1), 4.0, A.mult)
+        tt(lf(14, 6), lf(12, 6), c("CSR", 13, 19), A.mult)
+        ts(u6(4), u6(3), 3, A.bitwise_and)
+        tt(lf(15, 6), lf(13, 6), u6(4), A.add)
+        tt(lf(16, 6), lf(15, 6), lf(14, 6), A.max)
+        copy(lu(3, 6), lf(16, 6))
+
+    def refill(t):
+        landed("AL%d" % t, "an%d" % t, (rank + 1 + t) % 8)
+        copy(ind(c("BK"), lu(3, 6)), c("AL%d" % t))
+
+    def update(t):
+        ts(lf(6), VL, 64.0, A.is_lt)
+        ts(lf(7), lf(3), 48.0, A.is_ge)
+        ts(lf(17), li(0), 1.0, A.add, 0.0, A.max)
+        tt(lf(8), lf(8), li(0), A.add)
+        tt(lf(9), lf(7), lf(6), A.mult)
+        ts(lf(17), lf(17), 31.0, A.mult, -16.0, A.add)
+        tt(lf(8), lf(8), c("DMK"), A.subtract)
+        VV = VL
+        if t == 2:
+            ts(li(12), VL, 12, A.bitwise_and)
+            tt(li(11), VL, li(12), A.subtract)
+            VV = li(11)
+        tt(lf(8), lf(8), lf(9), A.mult)
+        tt(lf(18), lf(17), VV, A.subtract)
+        tt(lf(8), lf(8), c("DMK"), A.add)
+        copy(lu(4), lf(8))
+        ts(lu(5), lf(8), 1.0, A.add)
+        copy(ind(c("MK"), lu(4)), c("ST%d" % (t + 1)))
+        tt(c("GV"), ind(lf(18), c("RI", 0, 12)), c("MSK16"), A.mult)
+        tt(c("NW"), ind(c("MK"), lu(5)), c("MASK"), A.mult)
+        tt(lf(19), lf(19), lf(9), A.mult)
+        scan(c("NS"), c("RST", 0, 192), c("NW"), 0.0, A.mult, A.add)
+        ts(lf(20), c("NS", 15, 192, 16), float(t + 1), A.not_equal)
+        tt(lf(20), lf(20), lf(19), A.mult)
+        tt(lf(20), lf(20), c("K1K"), A.add)
+        copy(lu(6), lf(20))
+        copy(ind(c("HF"), lu(6)), c("GV"))
+
+    o64 = lambda k: c("OI", 64 * k, 64 * k + 64)
+
+    def heads_out():
+        for j in range(16):
+            mm(c("b1", 0, 64), c("SELJ", 128 * j, 128 * j + 128), c("HF", 64 * j, 64 * j + 64), j == 0, j == 15)
+        copy(o64(2), c("b1", 0, 64))
+        ts(o64(0), o64(2), 15.0, A.add)
+        ts(o64(1), o64(0), 4, A.arith_shift_right)
+        copy(c("OF", 0, 64), o64(1))
+        dma("s", "yf", ext(T.yf[:]), c("OF", 0, 64))
+        ts(o64(0), o64(1), 15.0, A.mult)
+        tt(o64(0), o64(0), o64(2), A.subtract)
+        ts(o64(3), o64(0), 3, A.bitwise_and)
+        copy(c("OF", 64, 128), o64(3))
+        dma("s", "yh", ext(T.yh[:]), c("OF", 64, 128))
+
+    for t in range(3):
+        places(t)
+        if t == 0:
+            consts_last()
+        else:
+            refill(t - 1)
+        pop_front(t)
+        if t == 0:
+            consts_tail()
+        pop_gathers(t)
+        if t < 2:
+            refill_list(t)
+            answer_front(t)
+            pop_dist(t)
+            answer_gathers(t)
+            answer_dist(t)
+            update(t)
+            pop_min(t)
+            pop_hot(t)
+            answer_list(t)
+            pop_move(t)
+            answer_send(t)
+            if t == 0:
+                consts_out()
+        else:
+            dma("s", "yz", ext(T.yz[:]), c("Z3"))
+            pop_dist(t)
+            update(t)
+            heads_out()
+            pop_min(t)
+            pop_hot(t)
+            pop_move(t)
+            copy(c("AFIN"), c("b5", 0, 192))
+            dma("s", "ya", ext(T.ya[:]), c("AFIN", p0=0, ps=16))
+
+    for i in settle(ops):
+        q, fn, rr, ww, sem, tot, us, lat = ops[i]
+        if q == "r":
+            hist[ww[0][0]] = [(ww[0][1], ww[0][2], True, "r", sem, tot, {sem: tot}, True)]
+        elif tot < 0:
+            need(q, rr, [], True)
+            fn()
+        elif sem:
+            need(q, rr, ww, True)
+            fn().then_inc(T.sem[sem], 16)
+            note(q, rr, ww, sem, tot, True)
+        else:
+            need(q, rr, ww, False)
+            count[q] += 1
+            fn().then_inc(T.sem[csem[q]], 1)
+            note(q, rr, ww, csem[q], count[q], False)
+
+    g.wait_ge(T.sem.sent, nsent[0])
+    for q in ("v", "t", "a", "g"):
+        g.wait_ge(T.sem[csem[q]], count[q])
+    for n in LOADS:
+        g.wait_ge(T.sem["d_" + n], 160 if n == "zero" else 16)

@@ -7,53 +7,52 @@ F = ActivationFunctionType
 
 SCRATCH = {}
 for _n, _c, _d in (
-    ("XS", 1024, "bfloat16"), ("SU", 1216, "int32"), ("BK", 4208, "bfloat16"), ("HFI", 1024, "int32"), ("HF", 1216, "bfloat16"),
-    ("MK", 9424, "bfloat16"), ("A0", 12, "int32"), ("aF", 12, "float32"), ("Z0", 192, "bfloat16"), ("Z1", 192, "bfloat16"),
-    ("Z2", 192, "bfloat16"), ("Z3", 192, "bfloat16"), ("ZQ0", 576, "int32"), ("ZQ1", 576, "int32"),
-    ("QL0", 96, "int32"), ("QL1", 96, "int32"), ("AL0", 96, "bfloat16"), ("AL1", 96, "bfloat16"),
-    ("ONE", 1536, "bfloat16"), ("A16", 192, "bfloat16"), ("A16F", 128, "float32"), ("BOT", 128, "bfloat16"),
-    ("BO", 128, "bfloat16"), ("BOH", 128, "float16"), ("BOHK", 128, "float16"),
-    ("B16", 128, "bfloat16"), ("BM16", 128, "bfloat16"), ("BN", 128, "bfloat16"), ("B64K", 128, "bfloat16"),
-    ("ID", 128, "bfloat16"), ("IDN", 128, "bfloat16"), ("IDH", 128, "float16"), ("IDHN", 128, "float16"), ("IDF", 128, "float32"),
-    ("KLH", 12, "float16"), ("L0", 128, "bfloat16"), ("L16", 128, "bfloat16"), ("U0", 128, "bfloat16"), ("U16", 128, "bfloat16"),
-    ("TRI0", 128, "bfloat16"), ("TRI", 128, "bfloat16"), ("ZER", 1178, "bfloat16"), ("SELJ", 2048, "bfloat16"),
-    ("DC", 6, "float32"), ("MASK", 192, "float32"), ("MSK16", 192, "float32"), ("RSTB", 256, "bfloat16"),
-    ("RST", 256, "float32"), ("RBIG", 256, "float32"), ("IC", 256, "bfloat16"), ("SEL", 1536, "bfloat16"), ("IOT", 32, "int32"),
-    ("RI", 16, "uint16"), ("R15", 16, "uint16"), ("CST", 20, "float32"), ("CSR", 20, "float32"), ("DMK", 12, "float32"),
-    ("K1K", 12, "float32"), ("MCOL", 1, "float32"), ("WU", 128, "float16"), ("WU2", 128, "float16"), ("OROW", 128, "float32"),
-    ("ON12", 12, "float32"), ("ST1", 192, "bfloat16"), ("ST2", 192, "bfloat16"), ("ST3", 192, "bfloat16"),
-    ("G0", 192, "float16"), ("ARH", 192, "float16"), ("W", 192, "float32"), ("AS", 192, "float32"), ("AO", 12, "uint16"),
-    ("HFG", 192, "bfloat16"), ("EQ", 1248, "bfloat16"), ("WV", 192, "float32"),
+    ("XS", 1024, "bfloat16"), ("SU", 2048, "int32"), ("BK", 4208, "bfloat16"), ("TAB", 1216, "float32"),
+    ("HX", 128, "int32"), ("HY", 128, "float32"), ("A0", 12, "int32"), ("aF", 16, "float32"),
+    ("Z0", 192, "bfloat16"), ("Z1", 192, "bfloat16"), ("Z2", 192, "bfloat16"), ("Z3", 192, "bfloat16"),
+    ("ZQ0", 576, "int32"), ("ZQ1", 576, "int32"), ("QS0", 12, "int32"), ("QS1", 12, "int32"), ("QL0", 12, "int32"), ("QL1", 12, "int32"),
+    ("UC0", 192, "int32"), ("UC1", 192, "int32"), ("RC0", 192, "int32"), ("RC1", 192, "int32"),
+    ("RZ0", 192, "bfloat16"), ("RZ1", 192, "bfloat16"), ("AL0", 96, "bfloat16"), ("AL1", 96, "bfloat16"),
+    ("ONE", 192, "bfloat16"), ("A16", 192, "bfloat16"), ("BIGR", 192, "bfloat16"), ("BOT", 128, "bfloat16"), ("BO", 128, "bfloat16"),
+    ("BK3", 128, "float16"), ("L0", 128, "bfloat16"), ("LK3", 128, "float16"), ("BMH", 128, "bfloat16"), ("BN", 128, "bfloat16"),
+    ("B1K", 128, "bfloat16"), ("ID", 128, "bfloat16"), ("IDN", 128, "bfloat16"), ("ID3", 128, "bfloat16"), ("L64", 192, "bfloat16"),
+    ("TRI", 128, "bfloat16"), ("ZWP", 128, "bfloat16"), ("ZWQ", 128, "bfloat16"),
+    ("SM", 48, "bfloat16"), ("DC", 6, "float32"), ("MASK", 192, "bfloat16"), ("MASKB", 96, "float32"), ("RBIG", 192, "bfloat16"),
+    ("IC", 128, "bfloat16"), ("OFR", 128, "bfloat16"), ("IOT", 32, "int32"), ("RI", 32, "uint16"), ("CI", 2, "uint16"),
+    ("CST", 16, "bfloat16"), ("CSR", 16, "bfloat16"), ("CF", 48, "float32"),
+    ("WU", 128, "bfloat16"), ("WU2", 128, "float16"), ("OROW", 128, "bfloat16"), ("LH", 2048, "bfloat16"),
+    ("ARH", 192, "float16"), ("AS", 192, "float32"), ("AO", 12, "uint16"), ("HFG", 192, "bfloat16"), ("EQ", 2304, "bfloat16"),
     ("SV", 192, "int32"), ("T1", 192, "bfloat16"), ("PKS", 192, "float32"), ("OFQ", 12, "uint16"),
-    ("ZS", 192, "float16"), ("SGM", 192, "float16"), ("SGU", 192, "uint16"), ("ZT", 256, "bfloat16"),
-    ("CG", 3072, "bfloat16"), ("AD", 3072, "bfloat16"), ("SK", 256, "float32"), ("KE", 256, "float32"), ("H", 256, "bfloat16"),
-    ("P", 192, "float16"), ("AFIN", 192, "float32"), ("NW", 192, "float32"), ("NS", 192, "float32"), ("GV", 192, "bfloat16"),
-    ("LF", 320, "float32"), ("LI", 160, "int32"), ("LU", 96, "uint16"), ("BLK", 12, "bfloat16"), ("SC", 12, "bfloat16"), ("PK12", 12, "float16"),
-    ("ZI", 96, "int32"), ("ZH", 96, "float16"), ("QW", 96, "float32"), ("QS", 96, "int32"), ("WQ", 96, "bfloat16"), ("WC", 96, "bfloat16"),
-    ("WT", 128, "bfloat16"), ("U5", 576, "int32"), ("COU", 96, "uint16"), ("COF", 96, "float32"), ("CA", 1536, "bfloat16"),
-    ("AA", 1536, "bfloat16"), ("KQ", 128, "int32"), ("K8", 8, "int32"),
-    ("LT", 128, "float32"), ("ANS0", 96, "bfloat16"), ("ANS1", 96, "bfloat16"), ("RW", 96, "float32"), ("RS", 96, "int32"),
-    ("OF", 128, "float32"), ("OI", 256, "int32"),
+    ("ZS", 192, "float16"), ("SGM", 192, "float16"), ("SGU", 192, "uint16"), ("CG", 3072, "bfloat16"), ("AD", 3072, "bfloat16"),
+    ("SK", 256, "float32"), ("KE", 256, "float32"), ("H", 256, "bfloat16"), ("P", 192, "float16"), ("AFIN", 192, "float32"),
+    ("NEWS", 192, "float32"), ("MOD", 192, "float32"),
+    ("LF", 256, "float32"), ("LI", 96, "int32"), ("LU", 96, "uint16"), ("WN", 32, "bfloat16"),
+    ("SC", 12, "bfloat16"), ("PK12", 12, "float16"),
+    ("ZH", 96, "bfloat16"), ("QW", 96, "float32"), ("RS", 96, "int32"), ("WQ", 96, "bfloat16"), ("WC", 96, "bfloat16"),
+    ("U5", 960, "int32"), ("COU", 96, "uint16"), ("COF", 96, "float16"), ("CA", 1536, "bfloat16"), ("AA", 1536, "bfloat16"),
+    ("KQ", 128, "int32"), ("K8", 8, "int32"), ("LT", 128, "float32"), ("ANS0", 96, "bfloat16"), ("ANS1", 96, "bfloat16"),
 ):
     SCRATCH[_n] = ("sbuf", [128, _c], _d)
 for _k in range(8):
     SCRATCH["b%d" % _k] = ("psum", [128, 512], "float32")
 
-LOADS = ["a0", "z0", "fl", "hd", "su", "gs", "xs", "zero", "yz", "ya", "yh", "yf"]
-SEMAPHORES = ["cv", "ct", "ca", "cg"] + ["d_" + n for n in LOADS] + ["q0", "q1", "an0", "an1", "sent"]
+LOADS = ["a0", "z0", "fl", "hd", "tf", "th", "su", "gs", "xs", "yz", "ya", "yh", "yf"]
+SEMAPHORES = ["cv", "ct", "ca", "cg"] + ["d_" + n for n in LOADS] + ["q0", "q1", "an0", "an1", "z0", "z1", "c0", "c1", "sent"]
 
-SCH = ((2, 3, 4, 5), (2, 3, 4, 5), (3, 4, 5))
-ANS_S = (1, 2)
-ANS_ORDER = (0, 2, 1)
+VG = (((), (), ()), ((), (), ()), ((), (), ()))
+VJ = ((16, 16, 8), (16, 16, 8), (16, 16, 0))
+ON_V = ()
+HF_AT = (10, 4, 4)
+BANK = {"pk": "b1", "new": "b0", "d": ("b0", "b1"), "dq": ("b5", "b2"), "k": ("b3", "b1")}
 
-CYC, GATHER, SCATTER, PE_US, DMA_US, WAKE_US, TOL_US = 0.00104, 1.56, 3.8, 0.00072, 2.5, 0.07, 0.04
-WAYS = ((1.0, 1.0, 1.0, 4.0), (1.25, 1.2, 1.0, 3.0), (0.9, 0.9, 1.2, 5.5))
-TRIES, MOVES, SEED = 300, 7000, 0
+CYC, GATHER, SCATTER, PE_US, WAKE_US, TOL_US = 0.00104, 1.56, 3.8, 0.00072, 0.07, 0.04
+WAYS = ((1.0, 1.0, 1.0, 3.0), (1.2, 1.2, 1.0, 2.2), (0.9, 0.9, 1.15, 4.0))
+TRIES, MOVES, SEED = 1500, 40000, 0
 BYTES = {"float32": 4, "int32": 4, "bfloat16": 2, "float16": 2, "uint16": 2}
 SETTLED = {}
 
 
-def settle(ops):
+def settle(ops, tags):
     if "order" in SETTLED:
         return SETTLED["order"]
     n = len(ops)
@@ -65,11 +64,19 @@ def settle(ops):
                 for (l2, h2, w2, j) in last.get(nm, ()):
                     over = h2 > lo and hi > l2
                     if j != i and (ps or ((w or w2) and over)):
-                        waits = ops[j][0] != q or sem or ops[j][4] or (w2 and not w and over)
+                        waits = ops[j][0] != q or sem or ops[j][4] or (w2 and over and not (w and q == "t"))
                         pred[i][j] = max(pred[i].get(j, 0.0), WAKE_US if waits else 0.0)
         for w, regs in ((False, rr), (True, ww)):
             for nm, lo, hi in regs:
+                if SCRATCH.get(nm, ("dram",))[0] == "psum":
+                    last[nm] = [e for e in last.get(nm, ()) if e[3] == i or (e[2] and ops[e[3]][0] != "t")][-4:]
+                elif w:
+                    last[nm] = [e for e in last.get(nm, ()) if not (lo <= e[0] and e[1] <= hi)]
                 last.setdefault(nm, []).append((lo, hi, w, i))
+    for q in "sa":
+        loads = [i for i, o in enumerate(ops) if o[0] == q and o[4] and tags[i] == "first"]
+        for j, i in zip(loads, loads[1:]):
+            pred[i].setdefault(j, -ops[j][7])
     pred = [sorted(p.items()) for p in pred]
     succ = [[] for _ in range(n)]
     for i in range(n):
@@ -112,17 +119,19 @@ def settle(ops):
                     ready[ops[k][0]].add(k)
         return order
 
+    qs = [o[0] for o in ops]
+
     def ends(order):
         tot = 0.0
         for cs in cost:
             done, free = [0.0] * n, {q: 0.0 for q in "vtagsr"}
             for i in order:
                 us, lat = cs[i]
-                s = free[ops[i][0]]
+                s = free[qs[i]]
                 for j, wk in pred[i]:
                     if done[j] + wk > s:
                         s = done[j] + wk
-                free[ops[i][0]] = s + us
+                free[qs[i]] = s + us
                 done[i] = s + us + lat
             tot += max(done)
         return tot / len(cost)
@@ -131,10 +140,20 @@ def settle(ops):
     prio = list(base)
     best = listed(base)
     end = ends(best)
+    parts = {}
+    for i, tg in enumerate(tags):
+        parts.setdefault(tg, []).append(i)
+    parts = list(parts.values())
     for _ in range(TRIES):
         p = list(prio)
-        for k in rng.integers(0, n, int(rng.integers(1, 25))):
-            p[int(k)] += float(rng.normal() * 3.0)
+        if rng.random() < 0.5:
+            for k in rng.integers(0, len(parts), int(rng.integers(1, 4))):
+                d = float(rng.normal() * 3.0)
+                for i in parts[int(k)]:
+                    p[i] += d
+        else:
+            for k in rng.integers(0, n, int(rng.integers(1, 12))):
+                p[int(k)] += float(rng.normal() * 3.0)
         o = listed(p)
         e = ends(o)
         if e <= end:
@@ -145,7 +164,7 @@ def settle(ops):
     cur, cend = list(best), end
     for step in range(MOVES):
         i = int(rng.integers(n))
-        if ops[i][0] == "r":
+        if qs[i] == "r":
             continue
         lo = max([pos[j] for j, wk in pred[i]], default=-1) + 1
         hi = min([pos[k] for k, wk in succ[i]], default=n) - 1
@@ -187,7 +206,7 @@ def rank_program(g, core, T, topo):
                 for (l2, h2, w2, q2, sem, val, clk, away2) in hist.get(nm, ()):
                     over = h2 > lo and hi > l2
                     if q2 == q and not away and not away2:
-                        if w2 and not w and over:
+                        if w2 and over and not (w and q == "t"):
                             toks.append((sem, val, clk))
                     elif ps or (over and (w or w2)):
                         toks.append((sem, val, clk))
@@ -218,15 +237,19 @@ def rank_program(g, core, T, topo):
             out += x[1] if isinstance(x[1], list) else [x[1]]
         return out
 
-    ops = []
+    ops, tags, part = [], [], ["first"]
+
+    def add(*op):
+        ops.append(op)
+        tags.append(part[0])
 
     def run(q, fn, reads, writes, us):
-        ops.append((q, fn, flat(reads), flat(writes), None, 0, us, 0.0))
+        add(q, fn, flat(reads), flat(writes), None, 0, us, 0.0)
 
-    def dma(q, name, out, in_, total=16):
+    def dma(q, name, out, in_, lat, ww=None):
         rr = [in_[1]] if in_[1] else []
-        ww = [out[1]] if out[1] else []
-        ops.append((q, lambda: eng[q].dma_start(out[0], in_[0]), rr, ww, "d_" + name, total, 0.06, DMA_US))
+        ww = ww or ([out[1]] if out[1] else [])
+        add(q, lambda: eng[q].dma_start(out[0], in_[0]), rr, ww, "d_" + name, 16, 0.06, lat)
 
     def c(name, lo=0, hi=None, step=1, p0=0, p1=128, ps=1):
         hi = SCRATCH[name][1][1] if hi is None else hi
@@ -237,8 +260,8 @@ def rank_program(g, core, T, topo):
             ap = t[p0:p1, lo:hi:step]
         return (ap, (name, lo, hi), len(range(lo, hi, step)), BYTES[SCRATCH[name][2]], SCRATCH[name][0])
 
-    def ind(win, off):
-        return (win[0].indirect(off[0]), [win[1], off[1]], 16 * off[2], 4, "list")
+    def ind(win, off, more=()):
+        return (win[0].indirect(off[0]), [win[1], off[1]] + list(more), 16 * off[2], 4, "list")
 
     def ext(ap):
         return (ap, None)
@@ -257,15 +280,18 @@ def rank_program(g, core, T, topo):
     def half(*xs):
         return 0.5 if all(x[3] == 2 for x in xs) else 1.0
 
-    def copy(out, in_):
+    def sides(out, ins):
         if out[4] == "list":
-            rd, wr = [in_, (0, out[1][1])], [(0, out[1][0])]
-        else:
-            rd, wr = [in_], [out]
+            return list(ins) + [(0, out[1][1])], [(0, out[1][0])]
+        return list(ins), [out]
+
+    def copy(out, in_):
+        rd, wr = sides(out, [in_])
         run("v", lambda: g.vector.tensor_copy(out[0], in_[0]), rd, wr, cyc(out, [in_], half(out, in_)))
 
     def tt(out, a, b, op):
-        run("v", lambda: g.vector.tensor_tensor(out[0], a[0], b[0], op), [a, b], [out],
+        rd, wr = sides(out, [a, b])
+        run("v", lambda: g.vector.tensor_tensor(out[0], a[0], b[0], op), rd, wr,
             cyc(out, [a, b], 1.0 if "psum" in (a[4], b[4]) else 2.0))
 
     def ts(out, a, s1, op0, s2=None, op1=None):
@@ -276,18 +302,30 @@ def rank_program(g, core, T, topo):
         else:
             run("v", lambda: g.vector.tensor_scalar(out[0], a[0], val(s1), val(s2), op0, op1), rd, [out], us)
 
-    def scan(out, d0, d1, init, o0, o1):
-        run("v", lambda: g.vector.tensor_tensor_scan(out[0], d0[0], d1[0], init, o0, o1), [d0, d1], [out], cyc(out, [d1], 1.0))
+    def least(out, keys):
+        d0 = c("RBIG", 0, out[2], p1=keys[0].shape[0])
+        run("v", lambda: g.vector.tensor_tensor_scan(out[0], d0[0], keys[0], 1e9, A.max, A.min), [d0, keys], [out], cyc(out, [keys], 1.0))
 
-    def fill(x, v):
-        run("v", lambda: g.vector.memset(x[0], v), [], [x], cyc(x, [x], half(x)))
+    def fill(x, v, more=()):
+        run("v", lambda: g.vector.memset(x[0], v), [], [x] + list(more), cyc(x, [x], half(x)))
 
-    def mm(out, lhsT, rhs, start, stop):
-        us = PE_US * max(64, rhs[2]) * (4 if rhs[3] == 4 else 1)
-        run("t", lambda: g.tensor.matmul(out[0], lhsT[0], rhs[0], start, stop), [lhsT, rhs], [out], us)
+    def mms(calls):
+        us = sum(PE_US * max(min(64, l[2]), r[2]) * (4 if r[3] == 4 else 1) for o, l, r, s0, s1 in calls)
+        run("t", lambda: [g.tensor.matmul(o[0], l[0], r[0], s0, s1) for o, l, r, s0, s1 in calls][-1],
+            [x for k in calls for x in k[1:3]], [k[0] for k in calls], us)
 
-    def act(out, in_, func, bias=0.0, scale=1.0):
-        run("a", lambda: g.scalar.activation(out[0], in_[0], func, bias=bias, scale=scale), [in_], [out], cyc(out, [in_], 1.0))
+    def mm(*call):
+        mms([call])
+
+    def move(name, out, in_):
+        if name in ON_V:
+            copy(out, in_)
+        else:
+            act(out, in_)
+
+    def act(out, in_, func=F.Copy, bias=0.0, scale=1.0):
+        rd = [in_] + [x for x in (bias, scale) if isinstance(x, tuple)]
+        run("a", lambda: g.scalar.activation(out[0], in_[0], func, bias=val(bias), scale=val(scale)), rd, [out], cyc(out, [in_], 1.0))
 
     def iota(out, pattern, base, cm):
         us = 0.13 + 2 * out[2] * CYC
@@ -299,392 +337,365 @@ def rank_program(g, core, T, topo):
     def asel(out, in_, pattern, cmp, fillv, base, cm):
         run("g", lambda: g.affine_select(out[0], in_[0], pattern, cmp, fillv, base, cm), [in_], [out], 0.17 + 2 * out[2] * CYC)
 
-    dma("s", "a0", c("A0"), ext(T.a0[:]))
-    dma("a", "z0", c("Z0"), ext(T.z0[:]))
-    fill(c("ONE", 0, 256), 1.0)
-    run("v", lambda: g.vector.memset(T.HFI[:], 0), [], [c("HFI"), (0, ("HFI1", 0, 1024))], 1024 * CYC)
-    dma("s", "fl", c("HFI", p0=0, ps=16), ext(T.fl0[:]))
-    ops.append(("s", lambda: g.sync.dma_start(T.HFI[1:128:16, :], T.hd0[:]), [], [("HFI1", 0, 1024)], "d_hd", 16, 0.06, DMA_US))
-    dma("s", "su", c("SU", 0, 1024), ext(T.su[:]))
-    dma("a", "gs", c("BK", 0, 4096), ext(T.gs[:]))
-    dma("s", "xs", c("XS"), ext(T.xs[:]))
+    TAB1 = ("TAB1", 0, 1)
+    dma("s", "a0", c("A0"), ext(T.a0[:]), 1.6)
+    dma("a", "hd", c("HX", 0, 64), ext(T.hd0[:]), 1.7)
+    dma("a", "fl", c("HX", 64, 128), ext(T.fl0[:]), 1.7)
+    dma("a", "z0", c("Z0"), ext(T.z0[:]), 1.8)
+    dma("s", "su", c("SU", 1024, 2048), ext(T.su[:]), 3.2)
+    dma("s", "xs", c("XS"), ext(T.xs[:]), 3.8)
+    fill(c("ONE"), 1.0)
+    fill(c("TAB"), 0.0, [(0, TAB1)])
+    copy(c("HY"), c("HX"))
+    dma("s", "tf", c("TAB", 0, 1024, p0=0, ps=16), c("HY", 64, 128), 1.9)
+    dma("s", "th", c("TAB", 0, 1024, p0=1, ps=16), c("HY", 0, 64), 1.9, [TAB1])
+    dma("s", "gs", c("BK", 16, 4112), ext(T.gs[:]), 4.5)
+    part[0] = "constants"
 
-    asel(c("A16", p1=16), c("ONE", 0, 192, p1=16), [[0, 12], [-1, 16]], A.is_equal, 0.0, 0, 1)
+    cf = lambda k, n=1: c("CF", k, k + n)
+    sm = lambda k: c("SM", 8 * k, 8 * k + 8)
+    LP, ODD, ROW = c("CSR", 0, 12), c("CSR", 12, 13), c("CSR", 13, 14)
+    KL, K1K, DUM, HW, THR, MCOL = cf(0, 12), cf(12, 12), cf(24, 6), cf(30), cf(31), cf(32)
+    BO8 = c("BO", 0, 128, 16)
+    asel(c("A16", p1=16), c("ONE", p1=16), [[0, 12], [-1, 16]], A.is_equal, 0.0, 0, 1)
     asel(c("BOT"), c("ONE", 0, 128), [[-16, 8], [0, 16]], A.is_ge, 0.0, 0, 1)
     asel(c("BO"), c("BOT"), [[16, 8], [0, 16]], A.is_ge, 0.0, 15, -1)
     iota(c("IOT", 0, 16), [[1, 16]], 0, 0)
     iota(c("IOT", 16, 32), [[16, 16]], 15, 0)
     asel(c("L0"), c("BO"), [[1, 128]], A.is_gt, 0.0, 0, -1)
-    asel(c("U0"), c("BO"), [[-1, 128]], A.is_ge, 0.0, 0, 1)
-    iota(c("CST", 0, 1, p1=16), [[0, 1]], 1, 2)
-    iota(c("CST", 1, 13, p1=16), [[16, 12]], 193, 1)
-    iota(c("CST", 13, 19, p1=16), [[16, 6]], 4112, 1)
-    fill(c("LF", 312, 313), 0.0)
-    asel(c("LF", 313, 314), c("LF", 312, 313), [[0, 1]], A.not_equal, 240.0, 0, 1)
-    asel(c("CST", 19, 20), c("LF", 313, 314), [[0, 1]], A.not_equal, -16.0, -1, 1)
-    asel(c("RSTB"), c("ONE", 0, 256), [[0, 16], [1, 16]], A.not_equal, 0.0, 0, 0)
-    asel(c("TRI0"), c("BO"), [[-1, 128]], A.is_gt, 0.0, 0, 1)
+    iota(c("CST", 0, 12, p1=16), [[16, 12]], 0, 1)
+    iota(c("CST", 12, 13, p1=16), [[0, 1]], 1, 2)
+    iota(c("CST", 13, 14, p1=16), [[0, 1]], 0, 1)
+    asel(c("TRI"), c("BO"), [[-1, 128]], A.is_gt, 0.0, 0, 1)
     asel(c("ID"), c("ONE", 0, 128), [[-1, 128]], A.is_equal, 0.0, 0, 1)
-    fill(c("ZER"), 0.0)
-    mm(c("b0", 0, 192), c("A16", 0, 128, p1=16), c("A16", p1=16), True, True)
-    copy(c("RI"), c("IOT", 0, 16))
-    copy(c("MASK"), c("b0", 0, 192))
-    copy(c("aF"), c("A0"))
-    copy(c("AO"), c("A0"))
-    tt(c("G0"), ind(c("aF"), c("RI", 0, 12)), c("MASK"), A.mult)
-    copy(c("BOH"), c("BO"))
-    copy(c("R15"), c("IOT", 16, 32))
-    mm(c("b5", 0, 192), c("BOH"), c("G0"), True, True)
-    act(c("L16"), c("L0"), F.Copy, scale=16.0)
-    act(c("U16"), c("U0"), F.Copy, scale=16.0)
-    act(c("B16"), c("BO"), F.Copy, scale=16.0)
-    act(c("BM16"), c("BO"), F.Copy, scale=-1.0 / 16)
-    act(c("A16F", p1=16), c("A16", 0, 128, p1=16), F.Copy)
-    mm(c("b2", 0, 20), c("A16F", p1=16), c("CST", p1=16), True, True)
-    act(c("CSR"), c("b2", 0, 20), F.Copy)
-    act(c("RST"), c("RSTB"), F.Copy)
-    act(c("TRI"), c("TRI0"), F.Copy, scale=-1.0)
-    act(c("BN"), c("BO"), F.Copy, scale=-256.0)
+    iota(c("SU", 0, 1024), [[1, 1024]], 0, 0)
+    iota(c("IC", p1=1), [[0, 8], [1, 16]], 0, 0)
+    iota(c("OROW"), [[0, 8], [2, 16]], 1, 0)
     for k in range(8):
-        dma("s", "zero", c("MK", 1178 * k, 1178 * k + 1178), c("ZER"), 160)
-    for k in range(2):
-        dma("s", "zero", c("SELJ", 1024 * k, 1024 * k + 1024), c("ZER", 0, 1024), 160)
-
-    KL = c("CSR", 1, 13)
-
-    def consts_mid():
-        run("v", lambda: g.vector.tensor_scalar(T.HF[:, 0:1024], T.HFI[:], T.CSR[:, 19:20], None, A.mult),
-            [c("HFI"), c("CSR", 19, 20), (0, ("HFI1", 0, 1024))], [c("HF", 0, 1024)], 1024 * CYC)
-        fill(c("ON12"), 1.0)
-        copy(c("IDH"), c("ID"))
-        ts(c("IDHN"), c("ID"), -1.0, A.mult)
-        copy(c("KLH"), KL)
-        ts(c("BOHK"), c("BO"), 1024.0, A.mult)
-        for n in ("ZQ0", "ZQ1"):
-            fill(c(n, 0, 96), 16128)
-        fill(c("BK", 4096, 4208), 0.0)
-        ts(c("K1K"), KL, 831.0, A.add)
-        fill(c("ONE", 256, 1536), 1.0)
-        iota(c("OROW"), [[0, 8], [2, 16]], 1, 0)
-        iota(c("IC", p1=1), [[0, 16], [1, 16]], 0, 0)
-        asel(c("SEL"), c("ONE"), [[-1, 96], [0, 16]], A.is_equal, 0.0, 0, 1)
-        act(c("IDN"), c("ID"), F.Copy, scale=-1.0)
-
-    def consts_last():
-        act(c("RBIG"), c("RST"), F.Copy, scale=-2e9, bias=1e9)
-        act(c("SK"), c("RST"), F.Copy)
-        act(c("KE"), c("RST"), F.Copy)
-        act(c("B64K"), c("BO"), F.Copy, scale=65536.0)
-        act(c("IDF"), c("ID"), F.Copy)
-        act(c("DC"), c("BO", 0, 96, 16), F.Copy)
-        act(c("MCOL"), c("CSR", 0, 1), F.Copy, scale=2048.0, bias=-2048.0 - 248.0 * 65536.0)
-        act(c("DMK"), KL, F.Copy, bias=9023.0)
-        ts(c("WU"), c("BO"), c("CSR", 0, 1), A.mult)
-        fill(c("K8"), 0)
-        fill(c("HF", 1024, 1216), 0.0)
-        tt(c("WU2"), c("WU"), c("OROW"), A.mult)
-
-    def consts_tail():
-        act(c("MSK16"), c("MASK"), F.Copy, scale=16.0)
-        for k in range(3):
-            act(c("ST%d" % (k + 1)), c("ONE", 0, 192), F.Copy, scale=float(k + 1))
-
-    def consts_out():
-        for j in range(16):
-            act(c("SELJ", 128 * j + j, 128 * j + 128, 16), c("BO", 0, 128, 16), F.Copy, scale=1.0 / 16)
+        act(c("LH", 192 * k, 192 * k + 192), c("ONE"), scale=0.0)
+    iota(cf(36, 2), [[1, 2]], 0, 1)
+    fill(c("OFR", p1=2), -248.0 * 65536.0)
+    iota(c("OFR", p1=1), [[0, 8], [4096, 16]], 2048, 0)
+    for name, col, scale in (("ZWP", (0, 1), -16.0), ("ZWQ", (2,), -65536.0)):
+        for nv in {v[x] for v in VJ for x in col} - ({0, 16} if name == "ZWP" else {0}):
+            asel(c(name), c("BO"), [[0, 8], [1, 16]], A.is_ge, 0.0, nv - 16, 0)
+            act(c(name), c(name), scale=scale)
+    mm(c("b0", 0, 192), c("A16", 0, 128, p1=16), c("A16", p1=16), True, True)
+    mm(c("b2", 0, 14), c("A16", 0, 128, p1=16), c("CST", 0, 14, p1=16), True, True)
+    copy(c("RI"), c("IOT"))
+    act(c("MASK"), c("b0", 0, 192))
+    act(c("BIGR", p1=16), c("A16", p1=16), scale=-2.0 ** 20, bias=2.0 ** 20)
+    act(c("CSR", 0, 14), c("b2", 0, 14))
+    fill(c("RBIG"), -1e9)
+    fill(c("RBIG", 0, 192, 16), 1e9)
+    fill(c("aF"), 0.0)
+    copy(c("aF", 0, 12), c("A0"))
+    tt(c("P"), ind(c("aF"), c("RI", 0, 12)), c("MASK"), A.mult)
+    ts(c("BK3"), c("BO"), 1451.0, A.mult)
+    ts(c("LK3"), c("L0"), 1451.0, A.mult)
+    ts(cf(33), ROW, 0.0, A.is_equal, -4096.0, A.mult)
+    ts(cf(34), ROW, 1.0, A.is_equal, 256.0, A.mult)
+    tt(HW, cf(33), cf(34), A.add)
+    act(c("BMH"), c("BO"), scale=HW)
+    act(THR, cf(34), scale=-1.0, bias=268.0)
+    act(KL, LP, bias=193.0)
+    act(K1K, LP, bias=1024.0)
+    act(DUM, c("CSR", 0, 6), bias=4096.0)
+    act(c("BN"), c("BO"), scale=-1.0)
+    act(c("B1K"), c("BO"), scale=1024.0)
+    act(c("IDN"), c("ID"), scale=-1.0)
+    act(c("ID3"), c("ID"), scale=3.0)
+    iota(c("L64", p1=1), [[64, 192]], 0, 0)
+    for k, v in enumerate((16.0, 32.0, -16.0, 65536.0, 131072.0, -65536.0)):
+        if k < 3 or k == 3 or max(v[2] for v in VJ) > 0:
+            act(sm(k), BO8, scale=v)
+    act(c("DC"), c("BO", 0, 96, 16))
+    act(c("MASKB"), c("MASK", 0, 96), scale=-2.0 ** 25, bias=2.0 ** 25)
+    act(cf(35), ODD)
+    act(c("WU"), c("BO"), scale=cf(35))
+    tt(c("WU2"), c("WU"), c("OROW"), A.mult)
+    act(MCOL, ROW, scale=127.0)
+    ts(c("CI"), cf(36, 2), MCOL, A.add)
+    for n in ("ZQ0", "ZQ1"):
+        fill(c(n, 0, 96), 63)
+    fill(c("BK", 0, 16), 0.0)
+    fill(c("BK", 4112, 4208), 0.0)
+    fill(c("WN"), 0.0)
+    fill(c("K8"), 0)
+    for n in ("SK", "KE"):
+        for h in range(2):
+            act(c(n, 128 * h, 128 * h + 128), c("ONE", 0, 128))
 
     def lf(k, n=12):
         return c("LF", 12 * k, 12 * k + n)
 
-    def li(k, n=12):
-        return c("LI", 12 * k, 12 * k + n)
+    def li(k, n=6):
+        return c("LI", 12 + 6 * k, 12 + 6 * k + n)
 
     def lu(k, n=12):
         return c("LU", 12 * k, 12 * k + n)
 
-    VL = c("SV", 15, 192, 16)
-
-    def aL(t):
-        return c("aF") if t == 0 else c("AS", 15, 192, 16)
-
+    VL, AL, NB = c("SV", 15, 192, 16), c("AS", 15, 192, 16), c("WN", 16, 28)
+    ROWA, ROWB = c("b4", 0, 192), c("b4", 192, 384)
     nsent = [0]
 
     def send(dst, out, in_, sem):
         rid, pid = topo.addr(T.cores[dst], core)
         nsent[0] += len(topo.engines(core, T.cores[dst]))
-        ops.append(("g", lambda: g.remote_dma(out, in_[0], T.sem[sem], T.sem.sent, pid, rid, topo.mask(core, T.cores[dst])),
-                    [in_[1]], [("sent " + sem, 0, 1)], None, -1, 0.3, 0.0))
+        add("g", lambda: g.remote_dma(out, in_[0], T.sem[sem], T.sem.sent, pid, rid, topo.mask(core, T.cores[dst])),
+            [in_[1]], [("sent " + sem, 0, 1)], None, -1, 0.3, 0.0)
 
     def landed(buf, sem, src):
         n = len(topo.engines(T.cores[src], core))
-        ops.append(("r", None, [("sent " + sem, 0, 1)], [(buf, 0, SCRATCH[buf][1][1])], sem, n, 0.0, 0.0))
+        add("r", None, [("sent " + sem, 0, 1)], [(buf, 0, SCRATCH[buf][1][1])], sem, n, 0.0, 0.0)
+
+    def big(out, start, stop):
+        mm(out, c("A16", 0, 128, p1=16), c("BIGR", p1=16), start, stop)
 
     def places(t):
         ask = t < 2
-        A5 = c("b5", 0, 192)
-        copy(c("ARH"), A5)
-        if t > 0:
-            tt(c("W"), A5, c("MASK"), A.mult)
-            scan(c("AS"), c("RST", 0, 192), c("W"), 0.0, A.mult, A.add)
-            copy(c("AO"), aL(t))
-        else:
-            consts_mid()
-        act(c("HFG"), ind(c("HF", 0, 1024), c("AO")), F.Copy)
-        V = c("b3", 0, 192)
-        o = 0
+        part[0] = "states%d" % t
+        big(ROWB, True, False)
+        mms([(ROWB, c("BO"), c("P"), False, True), (ROWA, c("BO"), c("P"), True, True)])
+        least(c("AS"), ROWB)
+        copy(c("ARH"), ROWA)
+        copy(c("AO"), AL)
+        copy(c("SGU"), ind(c("SU", 1024, 2048), c("AO")))
+        act(c("HFG"), ind(c("TAB", 0, 1024), c("AO"), [TAB1] if t == 0 else []))
+        act(lf(0), AL, scale=4.0, bias=16.0)
+        part[0] = "places%d" % t
+        W = ROWA
+        big(W, True, False)
         for k in range(12):
-            n = 192 - 16 * k
-            col = c("aF", k, k + 1) if t == 0 else c("AS", 16 * k + 15, 16 * k + 16)
-            ts(c("EQ", o, o + n), c("ARH", 16 * k, 192), col, A.is_equal)
-            if k == 0:
-                mm(V, c("L16"), c("EQ", 0, 192), True, False)
-                mm(c("b3", 16, 192), c("U16"), c("EQ", 16, 192), False, False)
-            else:
-                mm(c("b3", 16 * k, 16 * k + 16), c("L16"), c("EQ", o, o + 16), False, False)
-                if k < 11:
-                    mm(c("b3", 16 * k + 16, 192), c("B16"), c("EQ", o + 16, o + n), False, False)
-            o += n
-        mm(V, c("BM16"), c("HFG"), False, True)
-        copy(c("SU", 1024, 1216), A5)
-        act(lf(1), aL(t), F.Copy, scale=4.0)
-        act(lf(8), aL(t), F.Copy, scale=9.0, bias=4.0)
-        tt(lf(19), aL(t), c("K1K"), A.subtract)
-        tt(c("WV"), V, c("MASK"), A.mult)
+            o = 192 * k
+            ts(c("EQ", o, o + 192), c("ARH"), c("AS", 16 * k + 15, 16 * k + 16), A.is_equal, 3.0, A.mult)
+            calls = [(c("b4", 16 * k, 16 * k + 16), c("LK3"), c("EQ", o + 16 * k, o + 16 * k + 16), False, k == 11)]
+            if k < 11:
+                calls.append((c("b4", 16 * k + 16, 192), c("BK3"), c("EQ", o + 16 * k + 16, o + 192), False, False))
+            mms(calls)
+            if k == HF_AT[t]:
+                mm(W, c("BMH"), c("HFG"), False, False)
+        least(c("SV"), W)
         if ask:
-            act(c("T1"), c("WV"), F.Relu, bias=63.0, scale=-1.0)
-            PK = c("b4", 0, 192)
-            mm(PK, c("ID"), c("Z%d" % t), True, False)
-            mm(PK, c("BOHK"), c("ARH"), False, False)
+            part[0] = "pack%d" % t
+            PK = c(BANK["pk"], 192, 384)
+            if "T1" in ON_V:
+                ts(c("T1"), W, 63.0 * 256, A.min, -1.0 / 256, A.mult)
+            else:
+                act(c("T1"), W, F.Relu, bias=63.0, scale=-1.0 / 256)
+            mms([(PK, c("ONE", 0, 128, p1=1), c("L64", p1=1), True, False), (PK, c("B1K"), c("ARH"), False, False)])
             mm(PK, c("BN"), c("T1"), False, True)
-            act(c("PKS"), PK, F.Copy, bias=256.0 * 1008.0)
-        scan(c("SV"), c("RST", 0, 192), c("WV"), 0.0, A.mult, A.add)
-        ts(c("BLK"), VL, 0.0, A.is_ge)
-        scan(c("SC"), c("ON12"), c("BLK"), 0.0, A.mult, A.add)
-        tt(c("PK12"), c("BLK"), KL, A.mult)
-        CUM = c("b6", 0, 12)
-        mm(CUM, c("TRI"), c("BLK"), True, False)
-        mm(CUM, c("BO"), c("SC"), False, False)
-        mm(CUM, c("IDH"), c("KLH"), False, False)
-        mm(CUM, c("IDHN"), c("PK12"), False, True)
-        ts(li(0), VL, 4, A.arith_shift_right)
-        tt(lf(21), c("BLK"), c("K1K"), A.mult)
-        act(lf(2), c("BLK"), F.Copy, scale=4096.0)
-        tt(li(1), li(0), VL, A.add)
-        tt(lf(21), lf(21), aL(t), A.max)
-        if ask:
-            ts(c("OFQ"), CUM, -1.0, A.add)
-            copy(ind(c("ZQ%d" % t), c("OFQ")), c("PKS"))
-        act(lf(3), CUM, F.Abs, bias=-144.5)
-        if ask:
-            send((rank + 1 + t) % 8, T["QL%d" % t][:], c("ZQ%d" % t, 0, 96), "q%d" % t)
-        ts(li(2), li(1), 3, A.bitwise_and)
-        copy(lu(7), lf(21))
-        tt(lf(4), lf(1), li(2), A.add)
-        tt(lf(5), lf(4), lf(2), A.max)
-        copy(lu(0), lf(5))
-
-    def pop_front(t):
-        Z, Z1 = c("Z%d" % t), c("Z%d" % (t + 1))
-        tt(c("ZS"), ind(c("BK", 0, 4112), lu(0)), Z, A.add)
-        copy(c("SGU"), ind(c("SU"), lu(7)))
-        ts(Z1, c("ZS"), 0.0, A.max, 255.0, A.min)
-        for h in range(2):
-            mm(c("b4", 128 * h, 128 * h + 128, p1=96), c("Z%d" % (t + 1), 96 * h, 96 * h + 96), c("IDN"), True, True)
-        act(c("ZT", p1=96), c("b4", 0, 256, p1=96), F.Copy)
-
-    def pop_gathers(t):
-        for k in range(6):
-            o, i = c("CG", 512 * k, 512 * k + 512), ind(c("XS"), c("SGU", 32 * k, 32 * k + 32))
-            if k in SCH[t]:
-                act(o, i, F.Copy)
+            b = -15.0 * 63 if "T1" in ON_V else 63.0
+            if "PKS" in ON_V:
+                ts(c("PKS"), PK, b, A.add)
             else:
-                copy(o, i)
-        for k in range(6):
-            D = c("b%d" % (k % 3))
-            mm(D, c("ZT", 128 * (k // 3), 128 * (k // 3) + 128, p1=96), c("SEL", 512 * (k % 3), 512 * (k % 3) + 512, p1=96), True, False)
-            mm(D, c("ID"), c("CG", 512 * k, 512 * k + 512), False, True)
-            act(c("AD", 512 * k, 512 * k + 512), D, F.Abs)
-        copy(c("SGM"), c("SGU"))
+                act(c("PKS"), PK, bias=b)
+        part[0] = "lists%d" % t
+        ts(NB, VL, 0.0, A.is_lt)
+        ts(li(0, 12), VL, 8, A.arith_shift_right, 3, A.bitwise_and)
+        ts(lf(1), VL, 0.0, A.is_lt, 1024.0, A.mult)
+        tt(lf(2), lf(0), li(0, 12), A.add)
+        tt(lf(4), AL, lf(1), A.add)
+        tt(lf(3), lf(2), NB, A.mult)
+        copy(lu(0, 24), lf(3, 24))
+        part[0] = "count%d" % t
+        run("v", lambda: g.vector.tensor_tensor_scan(T.SC[:], T.ONE[:, 0:12], NB[0], 0.0, A.mult, A.subtract),
+            [c("ONE", 0, 12), NB], [c("SC")], 64 * CYC)
+        tt(c("PK12"), NB, KL, A.mult)
+        CUM = c("b7", 0, 12)
+        mms([(CUM, c("ID"), LP, True, False), (CUM, c("TRI"), NB, False, False)])
+        mms([(CUM, c("BO"), c("SC"), False, False), (CUM, c("ID"), c("PK12"), False, True)])
+        if ask:
+            ZQ, QS, PL = "ZQ%d" % t, "QS%d" % t, c("RS", 15, 96, 16)
+            copy(c("OFQ"), CUM)
+            copy(ind(c(ZQ), c("OFQ")), c("PKS"))
+            tt(c("QW"), c(ZQ, 0, 96), c("MASKB"), A.add)
+            least(c("RS"), c("QW"))
+            ts(c(QS, 0, 6), PL, 6, A.arith_shift_right, 255, A.bitwise_and)
+            ts(c(QS, 6, 12), PL, 14, A.arith_shift_right)
+            send((rank + 1 + t) % 8, T["QL%d" % t][:], c(QS), "q%d" % t)
+        part[0] = "update%d" % t
+        ts(lf(5), CUM, 95.5, A.is_lt)
 
-    def pop_dist(t):
-        for h in range(2):
-            b = ("b3", "b4")[h]
-            mm(c(b, 0, 128, p1=96), c("ONE", 0, 96, p1=1), c("IC", 0, 128, p1=1), True, False)
-            for i in range(16):
-                mm(c(b, i, 128, 16, p1=96), c("AD", 1536 * h + i, 1536 * h + 1536, 16), c("B16", 0, 128, 16), False, i == 15)
-
-    def pop_min(t):
-        for h in range(2):
-            b = ("b3", "b4")[h]
-            act(c("KE", 128 * h, 128 * h + 128, p1=96), c(b, 0, 128, p1=96), F.Copy)
-            scan(c("SK", 128 * h, 128 * h + 128, p1=96), c("RBIG", 0, 128, p1=96), c(b, 0, 128, p1=96), 1e9, A.max, A.min)
-
-    def pop_hot(t):
-        tt(c("H"), ind(c("SK"), c("R15")), c("KE"), A.is_equal)
-        for h in range(2):
-            mm(c("b7", 96 * h, 96 * h + 96), c("H", 128 * h, 128 * h + 128, p1=96), c("ID", 0, 96, p1=96), True, True)
-
-    def pop_move(t):
-        tt(c("P"), c("b7", 0, 192), c("SGM"), A.mult)
-        mm(c("b5", 0, 192), c("BOH"), c("P"), True, True)
-
-    def answer_front(t):
-        QL = "QL%d" % t
-        landed(QL, "q%d" % t, (rank - 1 - t) % 8)
-        u = lambda k: c("U5", 96 * k, 96 * k + 96)
-        ts(c("ZI"), c(QL), 255, A.bitwise_and)
-        copy(c("ZH"), c("ZI"))
-        tt(c("QW"), c(QL), c("MASK", 0, 96), A.mult)
-        scan(c("QS"), c("RST", 0, 96), c("QW"), 0.0, A.mult, A.add)
-        mm(c("b7", 0, 96), c("WU"), c("ZH"), True, True)
-        mm(c("b7", 96, 192), c("WU2"), c("ZH"), True, True)
-        ts(li(3, 6), c("QS", 15, 96, 16), 14, A.arith_shift_right)
-        copy(lu(1, 6), li(3, 6))
-        tt(c("WQ"), ind(c("XS"), lu(1, 6)), c("ZI"), A.subtract)
-        copy(u(0), c("b7", 0, 96))
-        ts(c("WC"), c("WQ"), -16.0, A.max, 15.0, A.min)
+    def candidates(t):
+        part[0] = "slots%d" % t
+        Z, UC = c("Z%d" % t), c("UC%d" % t)
+        u = lambda k: c("U5", 192 * k, 192 * k + 192)
+        send((rank + 1 + t) % 8, T["RZ%d" % t][:], Z, "z%d" % t)
+        mms([(c("b6", 0, 192), c("WU"), Z, True, True), (c("b6", 192, 384), c("WU2"), Z, True, True)])
+        copy(u(0), c("b6", 0, 192))
         ts(u(1), u(0), 4095, A.bitwise_and)
-        mm(c("b6", 128, 256, p1=96), c("WC"), c("IDN"), True, True)
-        act(c("WT", p1=96), c("b6", 128, 256, p1=96), F.Copy)
         tt(u(2), u(1), u(1), A.mult)
         ts(u(3), u(2), 5, A.arith_shift_right)
-        tt(u(4), c("b7", 96, 192), u(3), A.add)
-        ts(u(5), u(4), 4095, A.bitwise_and)
-        copy(c("COU"), u(5))
+        tt(u(4), c("b6", 192, 384), u(3), A.add)
+        ts(UC, u(4), 4095, A.bitwise_and)
+        send((rank + 1 + t) % 8, T["RC%d" % t][:], UC, "c%d" % t)
 
-    def answer_gathers(t):
+    def pop_front(t):
+        part[0] = "front%d" % t
+        Z, Z1 = c("Z%d" % t), c("Z%d" % (t + 1))
+        tt(c("ZS"), ind(c("BK", 0, 4112), lu(0)), Z, A.add)
+        ts(Z1, c("ZS"), 0.0, A.max, 255.0, A.min)
+        if VJ[t][0] or VJ[t][1]:
+            mm(c("b7", 16, 208), c("ID"), Z1, True, True)
+        copy(c("SGM"), ind(c("SU"), lu(1)))
+
+    def gathers(out, o, win, offs, p, mine):
         for k in range(3):
-            o, i = c("CA", 512 * k, 512 * k + 512), ind(c("BK", 0, 4096), c("COU", 32 * k, 32 * k + 32))
-            if k in ANS_S:
-                act(o, i, F.Copy)
+            part[0] = "gather %s %d %d %s" % (out, o, k, part[0][-1])
+            a, b = c(out, o + 512 * k, o + 512 * k + 512), ind(win, c(offs, p + 32 * k, p + 32 * k + 32))
+            if k in mine:
+                copy(a, b)
             else:
-                copy(o, i)
-        ts(c("COF"), c("U5", 480, 576), c("MCOL"), A.add)
-        for k in ANS_ORDER:
-            D = c("b%d" % k)
-            mm(D, c("WT", p1=96), c("SEL", 512 * k, 512 * k + 512, p1=96), True, False)
-            mm(D, c("ID"), c("CA", 512 * k, 512 * k + 512), False, True)
-            act(c("AA", 512 * k, 512 * k + 512), D, F.Abs)
+                act(a, b)
 
-    def answer_dist(t):
-        mm(c("b6", 0, 128, p1=96), c("COF"), c("IDF"), True, False)
-        for m in range(16):
-            mm(c("b6", m, 128, 16, p1=96), c("AA", m, 1536, 16), c("B64K", 0, 128, 16), False, m == 15)
+    def sizes(src, dst, o, z, zp, banks, nv, keys, wts):
+        col = lambda j: c(src, o + j, o + 1536, 16)
+        blk = lambda j, n=1: c(dst, o + 96 * j, o + 96 * (j + n))
+        key = lambda j: c(keys[0], keys[1] + j, keys[1] + 128, 16, p1=96)
+        ns = 16 - nv
+        nb = -(-ns // 5)
+        cuts = [ns * b // nb for b in range(nb + 1)] if ns else [0]
+        todo = []
+        for b in range(nb):
+            bank = banks[0] if len(banks) == 1 else banks.pop(0)
+            if len(banks) > 0 and bank not in banks:
+                banks.append(bank)
+            calls = []
+            for j in range(cuts[b], cuts[b + 1]):
+                D = c(bank, 96 * (j - cuts[b]), 96 * (j - cuts[b] + 1))
+                calls += [(D, c("IDN"), z, True, False), (D, c("ID"), col(j), False, True)]
+            mms(calls)
+            n = cuts[b + 1] - cuts[b]
+            act(blk(cuts[b], n), c(bank, 0, 96 * n), F.Abs)
+            todo.append([(key(j), blk(j), sm(wts)) for j in range(cuts[b], cuts[b + 1])])
+        for j in range(ns, 16):
+            tt(blk(j), col(j), zp, A.max)
+        early = [[(key(j), col(j), sm(wts + 2)) for j in range(ns, 16)]] if nv else []
+        if nv and (ns or wts):
+            early.insert(1 - wts // 3, [(c(keys[0], keys[1], keys[1] + 128, p1=96), z, c("ZWQ" if wts else "ZWP"))])
+        late = [[(key(j), blk(j), sm(wts + 1)) for j in range(j0, min(16, j0 + 4))] for j0 in range(ns, 16, 4)]
+        mixed = []
+        while todo or late:
+            mixed += late[:1] + todo[:1]
+            late, todo = late[1:], todo[1:]
+        return early + mixed
 
-    def answer_list(t):
-        scan(c("KQ", p1=96), c("RBIG", 0, 128, p1=96), c("b6", 0, 128, p1=96), 1e9, A.max, A.min)
+    def summed(todo):
+        for x, calls in enumerate(todo):
+            mms([(o, l, r, x == 0 and y == 0, x == len(todo) - 1 and y == len(calls) - 1) for y, (o, l, r) in enumerate(calls)])
+
+    def pop_half(t, h, banks):
+        part[0] = "half%d%d" % (h, t)
+        z = c("Z%d" % (t + 1), 96 * h, 96 * h + 96)
+        todo = sizes("CG", "AD", 1536 * h, z, c("b7", 16 + 96 * h, 112 + 96 * h), banks, VJ[t][h], (BANK["k"][h], 128 * h), 0)
+        K = c(BANK["k"][h], 128 * h, 128 * h + 128, p1=96)
+        summed([[(K, c("ONE", 0, 96, p1=1), c("IC", p1=1))]] + todo)
+        least(c("SK", 128 * h, 128 * h + 128, p1=96), K)
+        act(c("KE", 128 * h, 128 * h + 128, p1=96), K)
+        tt(c("H", 128 * h, 128 * h + 128), ind(c("SK", 128 * h, 128 * h + 128), c("RI", 16, 24)), c("KE", 128 * h, 128 * h + 128), A.is_equal)
+
+    def pop_move(t):
+        for h in range(2):
+            mm(c("b3", 256 + 96 * h, 352 + 96 * h), c("H", 128 * h, 128 * h + 128, p1=96), c("ID", 0, 96, p1=96), True, True)
+        tt(c("P"), c("b3", 256, 448), c("SGM"), A.mult)
+
+    def answer_front(t):
+        part[0] = "asked%d" % t
+        for buf, sem in (("QL", "q"), ("RZ", "z"), ("RC", "c")):
+            landed("%s%d" % (buf, t), "%s%d" % (sem, t), (rank - 1 - t) % 8)
+        copy(lu(2), c("QL%d" % t))
+        copy(c("COU"), ind(c("RC%d" % t), lu(2, 6)))
+        move("ZH", c("ZH"), ind(c("RZ%d" % t), lu(2, 6)))
+        tt(c("WQ"), ind(c("XS"), c("LU", 30, 36)), c("ZH"), A.subtract)
+        ts(c("WC"), c("WQ"), -16.0, A.max, 15.0, A.min)
+        ts(c("COF"), c("COU"), -2048.0, A.add)
+
+    def answer(t):
+        part[0] = "answer%d" % t
+        nv = VJ[t][2]
+        dq = list(BANK["dq"])
+        if nv:
+            mm(c(dq[-1], 0, 96), c("ID"), c("WC"), True, True)
+        todo = sizes("CA", "AA", 0, c("WC"), c(dq[-1], 0, 96), dq[:-1] if nv else dq, nv, ("b6", 0), 3)
+        K = c("b6", 0, 128, p1=96)
+        low = [[(K, c("ONE", 0, 96, p1=2), c("OFR", p1=2)), (K, c("COF"), c("ID"))]]
+        summed(todo + low if nv else low + todo)
+        least(c("KQ", p1=96), K)
         ts(c("K8", p1=96), c("KQ", 15, 128, 16, p1=96), 4095, A.bitwise_and)
         tt(c("LT"), ind(c("K8"), c("RI", 0, 8)), c("MASK", 0, 128), A.mult)
         mm(c("b6", 256, 262), c("LT", p1=96), c("DC", p1=96), True, True)
-
-    def answer_send(t):
-        copy(lu(2, 6), c("b6", 256, 262))
+        copy(lu(3, 6), c("b6", 256, 262))
         ANS = c("ANS%d" % t)
-        copy(ANS, ind(c("BK", 0, 4096), lu(2, 6)))
+        move("ANS", ANS, ind(c("BK", 16, 4112), lu(3, 6)))
         send((rank - 1 - t) % 8, T["AL%d" % t][:], ANS, "an%d" % t)
 
     def refill_list(t):
-        u6 = lambda k: c("LI", 48 + 6 * k, 54 + 6 * k)
-        tt(c("RW"), c("ZQ%d" % t, 0, 96), c("MASK", 0, 96), A.mult)
-        scan(c("RS"), c("RST", 0, 96), c("RW"), 0.0, A.mult, A.add)
+        part[0] = "where%d" % t
         PL = c("RS", 15, 96, 16)
-        ts(u6(0), PL, 8, A.arith_shift_right, 63, A.bitwise_and)
-        ts(u6(1), PL, 14, A.arith_shift_right)
-        ts(u6(2), u6(0), 4, A.arith_shift_right)
-        ts(lf(12, 6), u6(0), 62.0, A.is_ge)
-        tt(u6(3), u6(0), u6(2), A.add)
-        ts(lf(13, 6), u6(1), 4.0, A.mult)
-        tt(lf(14, 6), lf(12, 6), c("CSR", 13, 19), A.mult)
-        ts(u6(4), u6(3), 3, A.bitwise_and)
-        tt(lf(15, 6), lf(13, 6), u6(4), A.add)
-        tt(lf(16, 6), lf(15, 6), lf(14, 6), A.max)
-        copy(lu(3, 6), lf(16, 6))
+        ts(li(2), PL, 12, A.arith_shift_right, 4092, A.bitwise_and)
+        ts(li(3), PL, 3, A.bitwise_and)
+        ts(li(4), PL, 63, A.bitwise_and)
+        tt(lf(10, 6), li(2), li(3), A.add)
+        ts(lf(11, 6), li(4), 60.0, A.is_ge, 8192.0, A.mult)
+        tt(lf(12, 6), lf(10, 6), lf(11, 6), A.add)
+        tt(lf(13, 6), lf(12, 6), DUM, A.min)
+        copy(lu(4, 6), lf(13, 6))
 
     def refill(t):
+        part[0] = "refill%d" % t
         landed("AL%d" % t, "an%d" % t, (rank + 1 + t) % 8)
-        copy(ind(c("BK"), lu(3, 6)), c("AL%d" % t))
+        copy(ind(c("BK", 16, 4208), lu(4, 6)), c("AL%d" % t))
 
     def update(t):
-        ts(lf(6), VL, 64.0, A.is_lt)
-        ts(lf(7), lf(3), 48.0, A.is_ge)
-        ts(lf(17), li(0), 1.0, A.add, 0.0, A.max)
-        tt(lf(8), lf(8), li(0), A.add)
-        tt(lf(9), lf(7), lf(6), A.mult)
-        ts(lf(17), lf(17), 31.0, A.mult, -16.0, A.add)
-        tt(lf(8), lf(8), c("DMK"), A.subtract)
-        VV = VL
-        if t == 2:
-            ts(li(12), VL, 12, A.bitwise_and)
-            tt(li(11), VL, li(12), A.subtract)
-            VV = li(11)
-        tt(lf(8), lf(8), lf(9), A.mult)
-        tt(lf(18), lf(17), VV, A.subtract)
-        tt(lf(8), lf(8), c("DMK"), A.add)
-        copy(lu(4), lf(8))
-        ts(lu(5), lf(8), 1.0, A.add)
-        copy(ind(c("MK"), lu(4)), c("ST%d" % (t + 1)))
-        tt(c("GV"), ind(lf(18), c("RI", 0, 12)), c("MSK16"), A.mult)
-        tt(c("NW"), ind(c("MK"), lu(5)), c("MASK"), A.mult)
-        tt(lf(19), lf(19), lf(9), A.mult)
-        scan(c("NS"), c("RST", 0, 192), c("NW"), 0.0, A.mult, A.add)
-        ts(lf(20), c("NS", 15, 192, 16), float(t + 1), A.not_equal)
-        tt(lf(20), lf(20), lf(19), A.mult)
-        tt(lf(20), lf(20), c("K1K"), A.add)
-        copy(lu(6), lf(20))
-        copy(ind(c("HF"), lu(6)), c("GV"))
+        part[0] = "update%d" % t
+        NEW = c(BANK["new"], 0, 192)
+        ts(lf(6), VL, 64.0 * 256, A.is_lt)
+        tt(lf(7), lf(5), lf(6), A.mult)
+        tt(c("WN", 0, 12), lf(7), NB, A.subtract)
+        copy(ind(c("LH"), c("CI")), c("WN"))
+        mm(NEW, c("ID3"), c("HFG"), True, False)
+        for k0 in range(0, 12, 4):
+            mms([(c(BANK["new"], 0, 16 * k + 16), c("LH", 128 * k, 128 * k + 128), c("EQ", 192 * k, 208 * k + 16), False, k == 11)
+                 for k in range(k0, k0 + 4)])
+        ts(li(5, 12), VL, 255, A.bitwise_and)
+        ts(lf(8), li(5, 12), 2048.0, A.mult)
+        tt(lf(9), lf(8), K1K, A.min)
+        tt(lf(8), lf(9), AL, A.max)
+        copy(lu(5), lf(8))
+        ts(c("MOD"), NEW, THR, A.is_ge, -4.0, A.mult)
+        act(c("NEWS"), NEW, scale=1.0 / 3)
+        tt(ind(c("TAB"), lu(5)), c("NEWS"), c("MOD"), A.add)
 
-    o64 = lambda k: c("OI", 64 * k, 64 * k + 64)
-
-    def heads_out():
-        for j in range(16):
-            mm(c("b1", 0, 64), c("SELJ", 128 * j, 128 * j + 128), c("HF", 64 * j, 64 * j + 64), j == 0, j == 15)
-        copy(o64(2), c("b1", 0, 64))
-        ts(o64(0), o64(2), 15.0, A.add)
-        ts(o64(1), o64(0), 4, A.arith_shift_right)
-        copy(c("OF", 0, 64), o64(1))
-        dma("s", "yf", ext(T.yf[:]), c("OF", 0, 64))
-        ts(o64(0), o64(1), 15.0, A.mult)
-        tt(o64(0), o64(0), o64(2), A.subtract)
-        ts(o64(3), o64(0), 3, A.bitwise_and)
-        copy(c("OF", 64, 128), o64(3))
-        dma("s", "yh", ext(T.yh[:]), c("OF", 64, 128))
-
+    candidates(0)
     for t in range(3):
         places(t)
-        if t == 0:
-            consts_last()
-        else:
+        banks = list(BANK["d"])
+        for h in range(2):
+            gathers("CG", 1536 * h, c("XS"), "SGU", 96 * h, VG[t][h])
+        if t > 0:
             refill(t - 1)
         pop_front(t)
         if t == 0:
-            consts_tail()
-        pop_gathers(t)
+            candidates(1)
+        update(t)
+        pop_half(t, 0, banks)
         if t < 2:
             refill_list(t)
             answer_front(t)
-            pop_dist(t)
-            answer_gathers(t)
-            answer_dist(t)
-            update(t)
-            pop_min(t)
-            pop_hot(t)
-            answer_list(t)
-            pop_move(t)
-            answer_send(t)
-            if t == 0:
-                consts_out()
-        else:
-            dma("s", "yz", ext(T.yz[:]), c("Z3"))
-            pop_dist(t)
-            update(t)
-            heads_out()
-            pop_min(t)
-            pop_hot(t)
-            pop_move(t)
-            copy(c("AFIN"), c("b5", 0, 192))
-            dma("s", "ya", ext(T.ya[:]), c("AFIN", p0=0, ps=16))
+            gathers("CA", 0, c("BK", 16, 4112), "COU", 0, VG[t][2])
+        pop_half(t, 1, banks)
+        pop_move(t)
+        if t < 2:
+            answer(t)
+    dma("s", "yz", ext(T.yz[:]), c("Z3"), 2.0)
+    dma("s", "yf", ext(T.yf[:]), c("TAB", 0, 1024, p0=0, ps=16), 2.0)
+    dma("s", "yh", ext(T.yh[:]), c("TAB", 0, 1024, p0=1, ps=16), 2.0)
+    mm(ROWA, c("BO"), c("P"), True, True)
+    move("AFIN", c("AFIN"), ROWA)
+    dma("s", "ya", ext(T.ya[:]), c("AFIN", p0=0, ps=16), 2.0)
 
-    for i in settle(ops):
+    for i in settle(ops, tags):
         q, fn, rr, ww, sem, tot, us, lat = ops[i]
         if q == "r":
             hist[ww[0][0]] = [(ww[0][1], ww[0][2], True, "r", sem, tot, {sem: tot}, True)]
@@ -705,4 +716,4 @@ def rank_program(g, core, T, topo):
     for q in ("v", "t", "a", "g"):
         g.wait_ge(T.sem[csem[q]], count[q])
     for n in LOADS:
-        g.wait_ge(T.sem["d_" + n], 160 if n == "zero" else 16)
+        g.wait_ge(T.sem["d_" + n], 16)

import numpy as np
from concourse.bass import DstId, RemoteDMATransfer
from concourse.mybir import dt, AluOpType, AxisListType, ActivationFunctionType

A = AluOpType
F = ActivationFunctionType

SCRATCH = {}
for _n, _c, _d in (
    ("XS", 1024, "bfloat16"), ("SU", 2048, "int32"), ("BK", 4208, "bfloat16"), ("TAB", 1216, "float32"),
    ("HX", 128, "int32"), ("HY", 128, "float32"), ("A0", 12, "int32"), ("aF", 16, "float32"),
    ("Z0", 192, "bfloat16"), ("Z1", 192, "bfloat16"), ("Z2", 192, "bfloat16"), ("Z3", 192, "bfloat16"),
    ("ZQ0", 576, "int32"), ("ZQ1", 576, "int32"), ("QS0", 12, "int32"), ("QS1", 12, "int32"), ("QL0", 12, "int32"), ("QL1", 12, "int32"),
    ("UC0", 192, "int32"), ("UC1", 192, "int32"), ("RC0", 192, "int32"), ("RC1", 192, "int32"),
    ("RZ0", 192, "bfloat16"), ("RZ1", 192, "bfloat16"), ("AL0", 96, "bfloat16"), ("AL1", 96, "bfloat16"),
    ("ONE", 192, "bfloat16"), ("A16", 192, "bfloat16"), ("BIGR", 192, "bfloat16"), ("BOT", 128, "bfloat16"), ("BO", 128, "bfloat16"),
    ("BK3", 128, "float16"), ("L0", 128, "bfloat16"), ("LK3", 128, "float16"), ("BMH", 128, "bfloat16"), ("BN", 128, "bfloat16"),
    ("B1K", 128, "bfloat16"), ("ID", 128, "bfloat16"), ("IDN", 128, "bfloat16"), ("ID3", 128, "bfloat16"), ("L64", 192, "bfloat16"),
    ("TRI", 128, "bfloat16"), ("ZWP", 128, "bfloat16"), ("ZWQ", 128, "bfloat16"),
    ("SM", 48, "bfloat16"), ("DC", 6, "float32"), ("MASK", 192, "bfloat16"), ("MASKB", 96, "float32"), ("RBIG", 192, "bfloat16"),
    ("IC", 128, "bfloat16"), ("OFR", 128, "bfloat16"), ("IOT", 32, "int32"), ("RI", 32, "uint16"), ("CI", 2, "uint16"),
    ("CST", 16, "bfloat16"), ("CSR", 16, "bfloat16"), ("CF", 48, "float32"),
    ("WU", 128, "bfloat16"), ("WU2", 128, "float16"), ("OROW", 128, "bfloat16"), ("LH", 2048, "bfloat16"),
    ("ARH", 192, "float16"), ("AS", 192, "float32"), ("AO", 12, "uint16"), ("HFG", 192, "bfloat16"), ("EQ", 2304, "bfloat16"),
    ("SV", 192, "int32"), ("T1", 192, "bfloat16"), ("PKS", 192, "float32"), ("OFQ", 12, "uint16"),
    ("ZS", 192, "float16"), ("SGM", 192, "float16"), ("SGU", 192, "uint16"), ("CG", 3072, "bfloat16"), ("AD", 3072, "bfloat16"),
    ("SK", 256, "float32"), ("KE", 256, "float32"), ("H", 256, "bfloat16"), ("P", 192, "float16"), ("AFIN", 192, "float32"),
    ("NEWS", 192, "float32"), ("MOD", 192, "float32"),
    ("LF", 256, "float32"), ("LI", 96, "int32"), ("LU", 96, "uint16"), ("WN", 32, "bfloat16"),
    ("SC", 12, "bfloat16"), ("PK12", 12, "float16"),
    ("ZH", 96, "bfloat16"), ("QW", 96, "float32"), ("RS", 96, "int32"), ("WQ", 96, "bfloat16"), ("WC", 96, "bfloat16"),
    ("U5", 960, "int32"), ("COU", 96, "uint16"), ("COF", 96, "float16"), ("CA", 1536, "bfloat16"), ("AA", 1536, "bfloat16"),
    ("KQ", 128, "int32"), ("K8", 8, "int32"), ("LT", 128, "float32"), ("ANS0", 96, "bfloat16"), ("ANS1", 96, "bfloat16"),
):
    SCRATCH[_n] = ("sbuf", [128, _c], _d)
for _k in range(8):
    SCRATCH["b%d" % _k] = ("psum", [128, 512], "float32")

LOADS = ["a0", "z0", "fl", "hd", "tf", "th", "su", "gs", "xs", "yz", "ya", "yh", "yf"]
SEMAPHORES = ["cv", "ct", "ca", "cg"] + ["d_" + n for n in LOADS] + ["q0", "q1", "an0", "an1", "z0", "z1", "c0", "c1", "sent"]

VG = (((), (), ()), ((), (), ()), ((), (), ()))
VJ = ((16, 16, 8), (16, 16, 8), (16, 16, 0))
ON_V = ()
HF_AT = (10, 4, 4)
BANK = {"pk": "b1", "new": "b0", "d": ("b0", "b1"), "dq": ("b5", "b2"), "k": ("b3", "b1")}

CYC, GATHER, SCATTER, PE_US, WAKE_US, TOL_US = 0.00104, 1.56, 3.8, 0.00072, 0.07, 0.04
WAYS = ((1.0, 1.0, 1.0, 3.0), (1.2, 1.2, 1.0, 2.2), (0.9, 0.9, 1.15, 4.0))
TRIES, MOVES, SEED = 1500, 40000, 0
BYTES = {"float32": 4, "int32": 4, "bfloat16": 2, "float16": 2, "uint16": 2}
SETTLED = {}


def settle(ops, tags):
    if "order" in SETTLED:
        return SETTLED["order"]
    n = len(ops)
    last, pred = {}, [{} for _ in range(n)]
    for i, (q, fn, rr, ww, sem, tot, us, lat) in enumerate(ops):
        for w, regs in ((False, rr), (True, ww)):
            for nm, lo, hi in regs:
                ps = SCRATCH.get(nm, ("dram",))[0] == "psum"
                for (l2, h2, w2, j) in last.get(nm, ()):
                    over = h2 > lo and hi > l2
                    if j != i and (ps or ((w or w2) and over)):
                        waits = ops[j][0] != q or sem or ops[j][4] or (w2 and over and not (w and q == "t"))
                        pred[i][j] = max(pred[i].get(j, 0.0), WAKE_US if waits else 0.0)
        for w, regs in ((False, rr), (True, ww)):
            for nm, lo, hi in regs:
                if SCRATCH.get(nm, ("dram",))[0] == "psum":
                    last[nm] = [e for e in last.get(nm, ()) if e[3] == i or (e[2] and ops[e[3]][0] != "t")][-4:]
                elif w:
                    last[nm] = [e for e in last.get(nm, ()) if not (lo <= e[0] and e[1] <= hi)]
                last.setdefault(nm, []).append((lo, hi, w, i))
    for q in "sa":
        loads = [i for i, o in enumerate(ops) if o[0] == q and o[4] and tags[i] == "first"]
        for j, i in zip(loads, loads[1:]):
            pred[i].setdefault(j, -ops[j][7])
    pred = [sorted(p.items()) for p in pred]
    succ = [[] for _ in range(n)]
    for i in range(n):
        for j, wk in pred[i]:
            succ[j].append((i, wk))
    cost = []
    for fv, fa, ft, fl in WAYS:
        f = {"v": fv, "a": fa, "t": ft}
        cost.append([(o[6] * f.get(o[0], 1.0), fl if o[5] < 0 else o[7]) for o in ops])
    base = [0.0] * n
    for i in range(n - 1, -1, -1):
        base[i] = cost[0][i][0] + max([0.0] + [cost[0][i][1] + wk + base[k] for k, wk in succ[i]])

    def listed(prio):
        left, at = [len(p) for p in pred], [0.0] * n
        free = {q: 0.0 for q in "vtagsr"}
        ready = {q: set() for q in "vtagsr"}
        for i in range(n):
            if left[i] == 0:
                ready[ops[i][0]].add(i)
        order = []
        while len(order) < n:
            bq, bs = None, 1e9
            for q, r in ready.items():
                if r:
                    s = max(free[q], min(at[i] for i in r))
                    if s < bs:
                        bq, bs = q, s
            i = max((k for k in ready[bq] if at[k] <= bs + TOL_US), key=lambda k: (prio[k], -k))
            ready[bq].remove(i)
            order.append(i)
            us, lat = cost[0][i]
            free[bq] = end = max(free[bq], at[i]) + us
            end += lat
            for k, wk in succ[i]:
                if end + wk > at[k]:
                    at[k] = end + wk
                left[k] -= 1
                if left[k] == 0:
                    ready[ops[k][0]].add(k)
        return order

    qs = [o[0] for o in ops]

    def ends(order):
        tot = 0.0
        for cs in cost:
            done, free = [0.0] * n, {q: 0.0 for q in "vtagsr"}
            for i in order:
                us, lat = cs[i]
                s = free[qs[i]]
                for j, wk in pred[i]:
                    if done[j] + wk > s:
                        s = done[j] + wk
                free[qs[i]] = s + us
                done[i] = s + us + lat
            tot += max(done)
        return tot / len(cost)

    rng = np.random.default_rng(SEED)
    prio = list(base)
    best = listed(base)
    end = ends(best)
    parts = {}
    for i, tg in enumerate(tags):
        parts.setdefault(tg, []).append(i)
    parts = list(parts.values())
    for _ in range(TRIES):
        p = list(prio)
        if rng.random() < 0.5:
            for k in rng.integers(0, len(parts), int(rng.integers(1, 4))):
                d = float(rng.normal() * 3.0)
                for i in parts[int(k)]:
                    p[i] += d
        else:
            for k in rng.integers(0, n, int(rng.integers(1, 12))):
                p[int(k)] += float(rng.normal() * 3.0)
        o = listed(p)
        e = ends(o)
        if e <= end:
            best, prio, end = o, p, e
    pos = [0] * n
    for x, i in enumerate(best):
        pos[i] = x
    cur, cend = list(best), end
    for step in range(MOVES):
        i = int(rng.integers(n))
        if qs[i] == "r":
            continue
        lo = max([pos[j] for j, wk in pred[i]], default=-1) + 1
        hi = min([pos[k] for k, wk in succ[i]], default=n) - 1
        lo, hi = max(lo, pos[i] - 150), min(hi, pos[i] + 150)
        if hi <= lo:
            continue
        x = int(rng.integers(lo, hi + 1))
        if x == pos[i]:
            continue
        o = list(cur)
        o.pop(pos[i])
        o.insert(x, i)
        e = ends(o)
        if e <= cend + 0.05 * (1.0 - step / MOVES) * float(rng.random()) ** 3:
            for y in range(min(x, pos[i]), max(x, pos[i]) + 1):
                pos[o[y]] = y
            cur, cend = o, e
            if e < end:
                best, end = o, e
    SETTLED["order"], SETTLED["end"] = best, end
    return best


def rank_program(g, core, T, topo):
    rank = T.rank_of(core)
    if rank is None:
        return
    eng = {"v": g.vector, "t": g.tensor, "a": g.scalar, "g": g, "s": g.sync}
    csem = {"v": "cv", "t": "ct", "a": "ca", "g": "cg"}
    count = {"v": 0, "t": 0, "a": 0, "g": 0}
    known = {q: {} for q in ("v", "t", "a", "g", "s", "r")}
    hist = {}

    def need(q, reads, writes, away):
        toks = []
        for w, regs in ((False, reads), (True, writes)):
            for nm, lo, hi in regs:
                ps = SCRATCH.get(nm, ("dram",))[0] == "psum"
                for (l2, h2, w2, q2, sem, val, clk, away2) in hist.get(nm, ()):
                    over = h2 > lo and hi > l2
                    if q2 == q and not away and not away2:
                        if w2 and over and not (w and q == "t"):
                            toks.append((sem, val, clk))
                    elif ps or (over and (w or w2)):
                        toks.append((sem, val, clk))
        k = known[q]
        toks.sort(key=lambda t: -t[1])
        for sem, val, clk in toks:
            if k.get(sem, 0) >= val:
                continue
            eng[q].wait_ge(T.sem[sem], val)
            for s, v in clk.items():
                if k.get(s, 0) < v:
                    k[s] = v

    def note(q, reads, writes, sem, val, away):
        clk = dict(known[q])
        clk[sem] = max(clk.get(sem, 0), val)
        for nm, lo, hi in writes:
            old = hist.get(nm, [])
            hist[nm] = [e for e in old if not (lo <= e[0] and e[1] <= hi)] + [(lo, hi, True, q, sem, val, clk, away)]
        for nm, lo, hi in reads:
            old = hist.setdefault(nm, [])
            hist[nm] = [e for e in old if not (not e[2] and e[3] == q and lo <= e[0] and e[1] <= hi and not e[7])] \
                + [(lo, hi, False, q, sem, val, clk, away)]

    def flat(xs):
        out = []
        for x in xs:
            out += x[1] if isinstance(x[1], list) else [x[1]]
        return out

    ops, tags, part = [], [], ["first"]

    def add(*op):
        ops.append(op)
        tags.append(part[0])

    def run(q, fn, reads, writes, us):
        add(q, fn, flat(reads), flat(writes), None, 0, us, 0.0)

    def dma(q, name, out, in_, lat, ww=None):
        rr = [in_[1]] if in_[1] else []
        ww = ww or ([out[1]] if out[1] else [])
        add(q, lambda: eng[q].dma_start(out[0], in_[0]), rr, ww, "d_" + name, 16, 0.06, lat)

    def c(name, lo=0, hi=None, step=1, p0=0, p1=128, ps=1):
        hi = SCRATCH[name][1][1] if hi is None else hi
        t = T[name]
        if step == 1:
            ap = t[p0:p1, lo:hi] if ps == 1 else t[p0:p1:ps, lo:hi]
        else:
            ap = t[p0:p1, lo:hi:step]
        return (ap, (name, lo, hi), len(range(lo, hi, step)), BYTES[SCRATCH[name][2]], SCRATCH[name][0])

    def ind(win, off, more=()):
        return (win[0].indirect(off[0]), [win[1], off[1]] + list(more), 16 * off[2], 4, "list")

    def ext(ap):
        return (ap, None)

    def val(x):
        return x[0] if isinstance(x, tuple) else x

    def cyc(out, ins, per):
        n = max(x[2] for x in ins)
        if out[4] == "list":
            return 0.05 + n * SCATTER * CYC
        if any(x[4] == "list" for x in ins):
            return 0.05 + n * GATHER * CYC
        return max(64, n * per) * CYC

    def half(*xs):
        return 0.5 if all(x[3] == 2 for x in xs) else 1.0

    def sides(out, ins):
        if out[4] == "list":
            return list(ins) + [(0, out[1][1])], [(0, out[1][0])]
        return list(ins), [out]

    def copy(out, in_):
        rd, wr = sides(out, [in_])
        run("v", lambda: g.vector.tensor_copy(out[0], in_[0]), rd, wr, cyc(out, [in_], half(out, in_)))

    def tt(out, a, b, op):
        rd, wr = sides(out, [a, b])
        run("v", lambda: g.vector.tensor_tensor(out[0], a[0], b[0], op), rd, wr,
            cyc(out, [a, b], 1.0 if "psum" in (a[4], b[4]) else 2.0))

    def ts(out, a, s1, op0, s2=None, op1=None):
        rd = [a] + [x for x in (s1, s2) if isinstance(x, tuple)]
        us = cyc(out, [a], half(out, a))
        if op1 is None:
            run("v", lambda: g.vector.tensor_scalar(out[0], a[0], val(s1), None, op0), rd, [out], us)
        else:
            run("v", lambda: g.vector.tensor_scalar(out[0], a[0], val(s1), val(s2), op0, op1), rd, [out], us)

    def least(out, keys):
        d0 = c("RBIG", 0, out[2], p1=keys[0].shape[0])
        run("v", lambda: g.vector.tensor_tensor_scan(out[0], d0[0], keys[0], 1e9, A.max, A.min), [d0, keys], [out], cyc(out, [keys], 1.0))

    def fill(x, v, more=()):
        run("v", lambda: g.vector.memset(x[0], v), [], [x] + list(more), cyc(x, [x], half(x)))

    def mms(calls):
        us = sum(PE_US * max(min(64, l[2]), r[2]) * (4 if r[3] == 4 else 1) for o, l, r, s0, s1 in calls)
        run("t", lambda: [g.tensor.matmul(o[0], l[0], r[0], s0, s1) for o, l, r, s0, s1 in calls][-1],
            [x for k in calls for x in k[1:3]], [k[0] for k in calls], us)

    def mm(*call):
        mms([call])

    def move(name, out, in_):
        if name in ON_V:
            copy(out, in_)
        else:
            act(out, in_)

    def act(out, in_, func=F.Copy, bias=0.0, scale=1.0):
        rd = [in_] + [x for x in (bias, scale) if isinstance(x, tuple)]
        run("a", lambda: g.scalar.activation(out[0], in_[0], func, bias=val(bias), scale=val(scale)), rd, [out], cyc(out, [in_], 1.0))

    def iota(out, pattern, base, cm):
        us = 0.13 + 2 * out[2] * CYC
        if SCRATCH[out[1][0]][2] == "int32":
            run("g", lambda: g.iota(out[0], pattern, base, cm), [], [out], us)
        else:
            run("g", lambda: g.iota(out[0], pattern, base, cm, allow_small_or_imprecise_dtypes=True), [], [out], us)

    def asel(out, in_, pattern, cmp, fillv, base, cm):
        run("g", lambda: g.affine_select(out[0], in_[0], pattern, cmp, fillv, base, cm), [in_], [out], 0.17 + 2 * out[2] * CYC)

    TAB1 = ("TAB1", 0, 1)
    dma("s", "a0", c("A0"), ext(T.a0[:]), 1.6)
    dma("a", "hd", c("HX", 0, 64), ext(T.hd0[:]), 1.7)
    dma("a", "fl", c("HX", 64, 128), ext(T.fl0[:]), 1.7)
    dma("a", "z0", c("Z0"), ext(T.z0[:]), 1.8)
    dma("s", "su", c("SU", 1024, 2048), ext(T.su[:]), 3.2)
    dma("s", "xs", c("XS"), ext(T.xs[:]), 3.8)
    fill(c("ONE"), 1.0)
    fill(c("TAB"), 0.0, [(0, TAB1)])
    copy(c("HY"), c("HX"))
    dma("s", "tf", c("TAB", 0, 1024, p0=0, ps=16), c("HY", 64, 128), 1.9)
    dma("s", "th", c("TAB", 0, 1024, p0=1, ps=16), c("HY", 0, 64), 1.9, [TAB1])
    dma("s", "gs", c("BK", 16, 4112), ext(T.gs[:]), 4.5)
    part[0] = "constants"

    cf = lambda k, n=1: c("CF", k, k + n)
    sm = lambda k: c("SM", 8 * k, 8 * k + 8)
    LP, ODD, ROW = c("CSR", 0, 12), c("CSR", 12, 13), c("CSR", 13, 14)
    KL, K1K, DUM, HW, THR, MCOL = cf(0, 12), cf(12, 12), cf(24, 6), cf(30), cf(31), cf(32)
    BO8 = c("BO", 0, 128, 16)
    asel(c("A16", p1=16), c("ONE", p1=16), [[0, 12], [-1, 16]], A.is_equal, 0.0, 0, 1)
    asel(c("BOT"), c("ONE", 0, 128), [[-16, 8], [0, 16]], A.is_ge, 0.0, 0, 1)
    asel(c("BO"), c("BOT"), [[16, 8], [0, 16]], A.is_ge, 0.0, 15, -1)
    iota(c("IOT", 0, 16), [[1, 16]], 0, 0)
    iota(c("IOT", 16, 32), [[16, 16]], 15, 0)
    asel(c("L0"), c("BO"), [[1, 128]], A.is_gt, 0.0, 0, -1)
    iota(c("CST", 0, 12, p1=16), [[16, 12]], 0, 1)
    iota(c("CST", 12, 13, p1=16), [[0, 1]], 1, 2)
    iota(c("CST", 13, 14, p1=16), [[0, 1]], 0, 1)
    asel(c("TRI"), c("BO"), [[-1, 128]], A.is_gt, 0.0, 0, 1)
    asel(c("ID"), c("ONE", 0, 128), [[-1, 128]], A.is_equal, 0.0, 0, 1)
    iota(c("SU", 0, 1024), [[1, 1024]], 0, 0)
    iota(c("IC", p1=1), [[0, 8], [1, 16]], 0, 0)
    iota(c("OROW"), [[0, 8], [2, 16]], 1, 0)
    for k in range(8):
        act(c("LH", 192 * k, 192 * k + 192), c("ONE"), scale=0.0)
    iota(cf(36, 2), [[1, 2]], 0, 1)
    fill(c("OFR", p1=2), -248.0 * 65536.0)
    iota(c("OFR", p1=1), [[0, 8], [4096, 16]], 2048, 0)
    for name, col, scale in (("ZWP", (0, 1), -16.0), ("ZWQ", (2,), -65536.0)):
        for nv in {v[x] for v in VJ for x in col} - ({0, 16} if name == "ZWP" else {0}):
            asel(c(name), c("BO"), [[0, 8], [1, 16]], A.is_ge, 0.0, nv - 16, 0)
            act(c(name), c(name), scale=scale)
    mm(c("b0", 0, 192), c("A16", 0, 128, p1=16), c("A16", p1=16), True, True)
    mm(c("b2", 0, 14), c("A16", 0, 128, p1=16), c("CST", 0, 14, p1=16), True, True)
    copy(c("RI"), c("IOT"))
    act(c("MASK"), c("b0", 0, 192))
    act(c("BIGR", p1=16), c("A16", p1=16), scale=-2.0 ** 20, bias=2.0 ** 20)
    act(c("CSR", 0, 14), c("b2", 0, 14))
    fill(c("RBIG"), -1e9)
    fill(c("RBIG", 0, 192, 16), 1e9)
    fill(c("aF"), 0.0)
    copy(c("aF", 0, 12), c("A0"))
    tt(c("P"), ind(c("aF"), c("RI", 0, 12)), c("MASK"), A.mult)
    ts(c("BK3"), c("BO"), 1451.0, A.mult)
    ts(c("LK3"), c("L0"), 1451.0, A.mult)
    ts(cf(33), ROW, 0.0, A.is_equal, -4096.0, A.mult)
    ts(cf(34), ROW, 1.0, A.is_equal, 256.0, A.mult)
    tt(HW, cf(33), cf(34), A.add)
    act(c("BMH"), c("BO"), scale=HW)
    act(THR, cf(34), scale=-1.0, bias=268.0)
    act(KL, LP, bias=193.0)
    act(K1K, LP, bias=1024.0)
    act(DUM, c("CSR", 0, 6), bias=4096.0)
    act(c("BN"), c("BO"), scale=-1.0)
    act(c("B1K"), c("BO"), scale=1024.0)
    act(c("IDN"), c("ID"), scale=-1.0)
    act(c("ID3"), c("ID"), scale=3.0)
    iota(c("L64", p1=1), [[64, 192]], 0, 0)
    for k, v in enumerate((16.0, 32.0, -16.0, 65536.0, 131072.0, -65536.0)):
        if k < 3 or k == 3 or max(v[2] for v in VJ) > 0:
            act(sm(k), BO8, scale=v)
    act(c("DC"), c("BO", 0, 96, 16))
    act(c("MASKB"), c("MASK", 0, 96), scale=-2.0 ** 25, bias=2.0 ** 25)
    act(cf(35), ODD)
    act(c("WU"), c("BO"), scale=cf(35))
    tt(c("WU2"), c("WU"), c("OROW"), A.mult)
    act(MCOL, ROW, scale=127.0)
    ts(c("CI"), cf(36, 2), MCOL, A.add)
    for n in ("ZQ0", "ZQ1"):
        fill(c(n, 0, 96), 63)
    fill(c("BK", 0, 16), 0.0)
    fill(c("BK", 4112, 4208), 0.0)
    fill(c("WN"), 0.0)
    fill(c("K8"), 0)
    for n in ("SK", "KE"):
        for h in range(2):
            act(c(n, 128 * h, 128 * h + 128), c("ONE", 0, 128))

    def lf(k, n=12):
        return c("LF", 12 * k, 12 * k + n)

    def li(k, n=6):
        return c("LI", 12 + 6 * k, 12 + 6 * k + n)

    def lu(k, n=12):
        return c("LU", 12 * k, 12 * k + n)

    VL, AL, NB = c("SV", 15, 192, 16), c("AS", 15, 192, 16), c("WN", 16, 28)
    ROWA, ROWB = c("b4", 0, 192), c("b4", 192, 384)
    nsent = [0]

    def send(dst, out, in_, sem):
        rid, pid = topo.addr(T.cores[dst], core)
        nsent[0] += len(topo.engines(core, T.cores[dst]))
        add("g", lambda: g.remote_dma(out, in_[0], T.sem[sem], T.sem.sent, pid, rid, topo.mask(core, T.cores[dst])),
            [in_[1]], [("sent " + sem, 0, 1)], None, -1, 0.3, 0.0)

    def landed(buf, sem, src):
        n = len(topo.engines(T.cores[src], core))
        add("r", None, [("sent " + sem, 0, 1)], [(buf, 0, SCRATCH[buf][1][1])], sem, n, 0.0, 0.0)

    def big(out, start, stop):
        mm(out, c("A16", 0, 128, p1=16), c("BIGR", p1=16), start, stop)

    def places(t):
        ask = t < 2
        part[0] = "states%d" % t
        big(ROWB, True, False)
        mms([(ROWB, c("BO"), c("P"), False, True), (ROWA, c("BO"), c("P"), True, True)])
        least(c("AS"), ROWB)
        copy(c("ARH"), ROWA)
        copy(c("AO"), AL)
        copy(c("SGU"), ind(c("SU", 1024, 2048), c("AO")))
        act(c("HFG"), ind(c("TAB", 0, 1024), c("AO"), [TAB1] if t == 0 else []))
        act(lf(0), AL, scale=4.0, bias=16.0)
        part[0] = "places%d" % t
        W = ROWA
        big(W, True, False)
        for k in range(12):
            o = 192 * k
            ts(c("EQ", o, o + 192), c("ARH"), c("AS", 16 * k + 15, 16 * k + 16), A.is_equal, 3.0, A.mult)
            calls = [(c("b4", 16 * k, 16 * k + 16), c("LK3"), c("EQ", o + 16 * k, o + 16 * k + 16), False, k == 11)]
            if k < 11:
                calls.append((c("b4", 16 * k + 16, 192), c("BK3"), c("EQ", o + 16 * k + 16, o + 192), False, False))
            mms(calls)
            if k == HF_AT[t]:
                mm(W, c("BMH"), c("HFG"), False, False)
        least(c("SV"), W)
        if ask:
            part[0] = "pack%d" % t
            PK = c(BANK["pk"], 192, 384)
            if "T1" in ON_V:
                ts(c("T1"), W, 63.0 * 256, A.min, -1.0 / 256, A.mult)
            else:
                act(c("T1"), W, F.Relu, bias=63.0, scale=-1.0 / 256)
            mms([(PK, c("ONE", 0, 128, p1=1), c("L64", p1=1), True, False), (PK, c("B1K"), c("ARH"), False, False)])
            mm(PK, c("BN"), c("T1"), False, True)
            b = -15.0 * 63 if "T1" in ON_V else 63.0
            if "PKS" in ON_V:
                ts(c("PKS"), PK, b, A.add)
            else:
                act(c("PKS"), PK, bias=b)
        part[0] = "lists%d" % t
        ts(NB, VL, 0.0, A.is_lt)
        ts(li(0, 12), VL, 8, A.arith_shift_right, 3, A.bitwise_and)
        ts(lf(1), VL, 0.0, A.is_lt, 1024.0, A.mult)
        tt(lf(2), lf(0), li(0, 12), A.add)
        tt(lf(4), AL, lf(1), A.add)
        tt(lf(3), lf(2), NB, A.mult)
        copy(lu(0, 24), lf(3, 24))
        part[0] = "count%d" % t
        run("v", lambda: g.vector.tensor_tensor_scan(T.SC[:], T.ONE[:, 0:12], NB[0], 0.0, A.mult, A.subtract),
            [c("ONE", 0, 12), NB], [c("SC")], 64 * CYC)
        tt(c("PK12"), NB, KL, A.mult)
        CUM = c("b7", 0, 12)
        mms([(CUM, c("ID"), LP, True, False), (CUM, c("TRI"), NB, False, False)])
        mms([(CUM, c("BO"), c("SC"), False, False), (CUM, c("ID"), c("PK12"), False, True)])
        if ask:
            ZQ, QS, PL = "ZQ%d" % t, "QS%d" % t, c("RS", 15, 96, 16)
            copy(c("OFQ"), CUM)
            copy(ind(c(ZQ), c("OFQ")), c("PKS"))
            tt(c("QW"), c(ZQ, 0, 96), c("MASKB"), A.add)
            least(c("RS"), c("QW"))
            ts(c(QS, 0, 6), PL, 6, A.arith_shift_right, 255, A.bitwise_and)
            ts(c(QS, 6, 12), PL, 14, A.arith_shift_right)
            send((rank + 1 + t) % 8, T["QL%d" % t][:], c(QS), "q%d" % t)
        part[0] = "update%d" % t
        ts(lf(5), CUM, 95.5, A.is_lt)

    def candidates(t):
        part[0] = "slots%d" % t
        Z, UC = c("Z%d" % t), c("UC%d" % t)
        u = lambda k: c("U5", 192 * k, 192 * k + 192)
        send((rank + 1 + t) % 8, T["RZ%d" % t][:], Z, "z%d" % t)
        mms([(c("b6", 0, 192), c("WU"), Z, True, True), (c("b6", 192, 384), c("WU2"), Z, True, True)])
        copy(u(0), c("b6", 0, 192))
        ts(u(1), u(0), 4095, A.bitwise_and)
        tt(u(2), u(1), u(1), A.mult)
        ts(u(3), u(2), 5, A.arith_shift_right)
        tt(u(4), c("b6", 192, 384), u(3), A.add)
        ts(UC, u(4), 4095, A.bitwise_and)
        send((rank + 1 + t) % 8, T["RC%d" % t][:], UC, "c%d" % t)

    def pop_front(t):
        part[0] = "front%d" % t
        Z, Z1 = c("Z%d" % t), c("Z%d" % (t + 1))
        tt(c("ZS"), ind(c("BK", 0, 4112), lu(0)), Z, A.add)
        ts(Z1, c("ZS"), 0.0, A.max, 255.0, A.min)
        if VJ[t][0] or VJ[t][1]:
            mm(c("b7", 16, 208), c("ID"), Z1, True, True)
        copy(c("SGM"), ind(c("SU"), lu(1)))

    def gathers(out, o, win, offs, p, mine):
        for k in range(3):
            part[0] = "gather %s %d %d %s" % (out, o, k, part[0][-1])
            a, b = c(out, o + 512 * k, o + 512 * k + 512), ind(win, c(offs, p + 32 * k, p + 32 * k + 32))
            if k in mine:
                copy(a, b)
            else:
                act(a, b)

    def sizes(src, dst, o, z, zp, banks, nv, keys, wts):
        col = lambda j: c(src, o + j, o + 1536, 16)
        blk = lambda j, n=1: c(dst, o + 96 * j, o + 96 * (j + n))
        key = lambda j: c(keys[0], keys[1] + j, keys[1] + 128, 16, p1=96)
        ns = 16 - nv
        nb = -(-ns // 5)
        cuts = [ns * b // nb for b in range(nb + 1)] if ns else [0]
        todo = []
        for b in range(nb):
            bank = banks[0] if len(banks) == 1 else banks.pop(0)
            if len(banks) > 0 and bank not in banks:
                banks.append(bank)
            calls = []
            for j in range(cuts[b], cuts[b + 1]):
                D = c(bank, 96 * (j - cuts[b]), 96 * (j - cuts[b] + 1))
                calls += [(D, c("IDN"), z, True, False), (D, c("ID"), col(j), False, True)]
            mms(calls)
            n = cuts[b + 1] - cuts[b]
            act(blk(cuts[b], n), c(bank, 0, 96 * n), F.Abs)
            todo.append([(key(j), blk(j), sm(wts)) for j in range(cuts[b], cuts[b + 1])])
        for j in range(ns, 16):
            tt(blk(j), col(j), zp, A.max)
        early = [[(key(j), col(j), sm(wts + 2)) for j in range(ns, 16)]] if nv else []
        if nv and (ns or wts):
            early.insert(1 - wts // 3, [(c(keys[0], keys[1], keys[1] + 128, p1=96), z, c("ZWQ" if wts else "ZWP"))])
        late = [[(key(j), blk(j), sm(wts + 1)) for j in range(j0, min(16, j0 + 4))] for j0 in range(ns, 16, 4)]
        mixed = []
        while todo or late:
            mixed += late[:1] + todo[:1]
            late, todo = late[1:], todo[1:]
        return early + mixed

    def summed(todo):
        for x, calls in enumerate(todo):
            mms([(o, l, r, x == 0 and y == 0, x == len(todo) - 1 and y == len(calls) - 1) for y, (o, l, r) in enumerate(calls)])

    def pop_half(t, h, banks):
        part[0] = "half%d%d" % (h, t)
        z = c("Z%d" % (t + 1), 96 * h, 96 * h + 96)
        todo = sizes("CG", "AD", 1536 * h, z, c("b7", 16 + 96 * h, 112 + 96 * h), banks, VJ[t][h], (BANK["k"][h], 128 * h), 0)
        K = c(BANK["k"][h], 128 * h, 128 * h + 128, p1=96)
        summed([[(K, c("ONE", 0, 96, p1=1), c("IC", p1=1))]] + todo)
        least(c("SK", 128 * h, 128 * h + 128, p1=96), K)
        act(c("KE", 128 * h, 128 * h + 128, p1=96), K)
        tt(c("H", 128 * h, 128 * h + 128), ind(c("SK", 128 * h, 128 * h + 128), c("RI", 16, 24)), c("KE", 128 * h, 128 * h + 128), A.is_equal)

    def pop_move(t):
        for h in range(2):
            mm(c("b3", 256 + 96 * h, 352 + 96 * h), c("H", 128 * h, 128 * h + 128, p1=96), c("ID", 0, 96, p1=96), True, True)
        tt(c("P"), c("b3", 256, 448), c("SGM"), A.mult)

    def answer_front(t):
        part[0] = "asked%d" % t
        for buf, sem in (("QL", "q"), ("RZ", "z"), ("RC", "c")):
            landed("%s%d" % (buf, t), "%s%d" % (sem, t), (rank - 1 - t) % 8)
        copy(lu(2), c("QL%d" % t))
        copy(c("COU"), ind(c("RC%d" % t), lu(2, 6)))
        move("ZH", c("ZH"), ind(c("RZ%d" % t), lu(2, 6)))
        tt(c("WQ"), ind(c("XS"), c("LU", 30, 36)), c("ZH"), A.subtract)
        ts(c("WC"), c("WQ"), -16.0, A.max, 15.0, A.min)
        ts(c("COF"), c("COU"), -2048.0, A.add)

    def answer(t):
        part[0] = "answer%d" % t
        nv = VJ[t][2]
        dq = list(BANK["dq"])
        if nv:
            mm(c(dq[-1], 0, 96), c("ID"), c("WC"), True, True)
        todo = sizes("CA", "AA", 0, c("WC"), c(dq[-1], 0, 96), dq[:-1] if nv else dq, nv, ("b6", 0), 3)
        K = c("b6", 0, 128, p1=96)
        low = [[(K, c("ONE", 0, 96, p1=2), c("OFR", p1=2)), (K, c("COF"), c("ID"))]]
        summed(todo + low if nv else low + todo)
        least(c("KQ", p1=96), K)
        ts(c("K8", p1=96), c("KQ", 15, 128, 16, p1=96), 4095, A.bitwise_and)
        tt(c("LT"), ind(c("K8"), c("RI", 0, 8)), c("MASK", 0, 128), A.mult)
        mm(c("b6", 256, 262), c("LT", p1=96), c("DC", p1=96), True, True)
        copy(lu(3, 6), c("b6", 256, 262))
        ANS = c("ANS%d" % t)
        move("ANS", ANS, ind(c("BK", 16, 4112), lu(3, 6)))
        send((rank - 1 - t) % 8, T["AL%d" % t][:], ANS, "an%d" % t)

    def refill_list(t):
        part[0] = "where%d" % t
        PL = c("RS", 15, 96, 16)
        ts(li(2), PL, 12, A.arith_shift_right, 4092, A.bitwise_and)
        ts(li(3), PL, 3, A.bitwise_and)
        ts(li(4), PL, 63, A.bitwise_and)
        tt(lf(10, 6), li(2), li(3), A.add)
        ts(lf(11, 6), li(4), 60.0, A.is_ge, 8192.0, A.mult)
        tt(lf(12, 6), lf(10, 6), lf(11, 6), A.add)
        tt(lf(13, 6), lf(12, 6), DUM, A.min)
        copy(lu(4, 6), lf(13, 6))

    def refill(t):
        part[0] = "refill%d" % t
        landed("AL%d" % t, "an%d" % t, (rank + 1 + t) % 8)
        copy(ind(c("BK", 16, 4208), lu(4, 6)), c("AL%d" % t))

    def update(t):
        part[0] = "update%d" % t
        NEW = c(BANK["new"], 0, 192)
        ts(lf(6), VL, 64.0 * 256, A.is_lt)
        tt(lf(7), lf(5), lf(6), A.mult)
        tt(c("WN", 0, 12), lf(7), NB, A.subtract)
        copy(ind(c("LH"), c("CI")), c("WN"))
        mm(NEW, c("ID3"), c("HFG"), True, False)
        for k0 in range(0, 12, 4):
            mms([(c(BANK["new"], 0, 16 * k + 16), c("LH", 128 * k, 128 * k + 128), c("EQ", 192 * k, 208 * k + 16), False, k == 11)
                 for k in range(k0, k0 + 4)])
        ts(li(5, 12), VL, 255, A.bitwise_and)
        ts(lf(8), li(5, 12), 2048.0, A.mult)
        tt(lf(9), lf(8), K1K, A.min)
        tt(lf(8), lf(9), AL, A.max)
        copy(lu(5), lf(8))
        ts(c("MOD"), NEW, THR, A.is_ge, -4.0, A.mult)
        act(c("NEWS"), NEW, scale=1.0 / 3)
        tt(ind(c("TAB"), lu(5)), c("NEWS"), c("MOD"), A.add)

    candidates(0)
    for t in range(3):
        places(t)
        banks = list(BANK["d"])
        for h in range(2):
            gathers("CG", 1536 * h, c("XS"), "SGU", 96 * h, VG[t][h])
        if t > 0:
            refill(t - 1)
        pop_front(t)
        if t == 0:
            candidates(1)
        update(t)
        pop_half(t, 0, banks)
        if t < 2:
            refill_list(t)
            answer_front(t)
            gathers("CA", 0, c("BK", 16, 4112), "COU", 0, VG[t][2])
        pop_half(t, 1, banks)
        pop_move(t)
        if t < 2:
            answer(t)
    dma("s", "yz", ext(T.yz[:]), c("Z3"), 2.0)
    dma("s", "yf", ext(T.yf[:]), c("TAB", 0, 1024, p0=0, ps=16), 2.0)
    dma("s", "yh", ext(T.yh[:]), c("TAB", 0, 1024, p0=1, ps=16), 2.0)
    mm(ROWA, c("BO"), c("P"), True, True)
    move("AFIN", c("AFIN"), ROWA)
    dma("s", "ya", ext(T.ya[:]), c("AFIN", p0=0, ps=16), 2.0)

    for i in settle(ops, tags):
        q, fn, rr, ww, sem, tot, us, lat = ops[i]
        if q == "r":
            hist[ww[0][0]] = [(ww[0][1], ww[0][2], True, "r", sem, tot, {sem: tot}, True)]
        elif tot < 0:
            need(q, rr, [], True)
            fn()
        elif sem:
            need(q, rr, ww, True)
            fn().then_inc(T.sem[sem], 16)
            note(q, rr, ww, sem, tot, True)
        else:
            need(q, rr, ww, False)
            count[q] += 1
            fn().then_inc(T.sem[csem[q]], 1)
            note(q, rr, ww, csem[q], count[q], False)

    g.wait_ge(T.sem.sent, nsent[0])
    for q in ("v", "t", "a", "g"):
        g.wait_ge(T.sem[csem[q]], count[q])
    for n in LOADS:
        g.wait_ge(T.sem["d_" + n], 16)
